import numpy as np
import ml_dtypes


def mxq(x, axis, fmt="e4m3"):
    dtype, down = {"e4m3": (ml_dtypes.float8_e4m3fn, 7), "e5m2": (ml_dtypes.float8_e5m2, 14)}[fmt]
    v = np.moveaxis(np.asarray(x, np.float32).astype(ml_dtypes.bfloat16).astype(np.float64), axis, -1)
    blocks = v.reshape(v.shape[:-1] + (-1, 32))
    amax = np.abs(blocks).max(-1, keepdims=True)
    byte = np.maximum(np.where(amax > 0, np.frexp(amax)[1] - 1 + 127, 0) - down, 1)
    scale = np.exp2(byte - 127.0)
    codes = (blocks / scale).astype(np.float32).astype(dtype).astype(np.float64)
    return np.moveaxis((codes * scale).reshape(v.shape), -1, axis)


WIDE = False


def mx_kscale(k):
    if not WIDE:
        return np.ones(k)
    levels = np.array([10, -10, 5, -5, 0])
    if k % 512:
        return np.exp2(np.random.permutation(np.resize(levels, k // 32))).repeat(32)
    a = np.empty((k // 512, 16))
    for p in range(k // 512):
        a[p, :8] = np.random.permutation(np.resize(levels, 8))
        for g in range(8):
            far = levels[np.abs(levels - a[p, g]) >= 10]
            a[p, g + 8] = far[np.random.randint(len(far))]
    return np.exp2(a.ravel()).repeat(32)


def f64(x):
    return np.asarray(x).astype(np.float64)


def striped(idx):
    return np.tile(idx.reshape(-1, 16).T, (8, 1)).astype(np.uint16)


def unstriped(offs):
    return offs[:16].T.reshape(-1).astype(np.int64)


E2M1 = np.array([0.0, 0.5, 1.0, 1.5, 2.0, 3.0, 4.0, 6.0, -0.0, -0.5, -1.0, -1.5, -2.0, -3.0, -4.0, -6.0])


def pack_weight(w, fmt):
    k, n = w.shape
    w = f64(np.asarray(w, np.float32).astype(ml_dtypes.bfloat16)).reshape(k // 32, 32, n)
    amax = np.abs(w).max(1)
    if fmt == "e4m3":
        byte = np.frexp(amax)[1] - 1 + 127 - 7
    else:
        mant, ex = np.frexp(amax / 6.0)
        byte = np.where(mant > 0.5, ex, ex - 1) + 127
    byte = np.clip(np.where(amax > 0, byte, 1), 1, 254)
    scaled = (w * np.exp2(127.0 - byte)[:, None, :]).reshape(k, n).astype(np.float32)
    by_word = np.ascontiguousarray(scaled.reshape(k // 512, 128, 4, n).transpose(0, 1, 3, 2))
    if fmt == "e4m3":
        words = by_word.astype(ml_dtypes.float8_e4m3fn).view(np.uint8)
    else:
        c = by_word.astype(ml_dtypes.float4_e2m1fn).view(np.uint8) & 0xF
        words = (c[..., 0::2] | (c[..., 1::2] << 4)).reshape(k // 512, 128, 2 * n)
    return np.ascontiguousarray(words), np.ascontiguousarray(byte.astype(np.uint8).reshape(k // 512, 16, n))


def unpack_weight(words, scales, fmt):
    g, _, n = scales.shape
    words = np.ascontiguousarray(words).reshape(g, 128, n, -1)
    if fmt == "e4m3":
        vals = words.view(ml_dtypes.float8_e4m3fn).astype(np.float64)
    else:
        nib = np.empty((g, 128, n, 4), np.uint8)
        nib[..., 0::2] = words & 0xF
        nib[..., 1::2] = words >> 4
        vals = E2M1[nib]
    vals = vals * np.repeat(np.exp2(scales.astype(np.float64) - 127.0), 8, axis=1)[..., None]
    return vals.transpose(0, 1, 3, 2).reshape(g * 512, n)


K, M, T, S = 1536, 512, 2048, 1024


def setup_inputs():
    n = np.random.standard_normal
    s = mx_kscale(K)[:, None]
    u = mx_kscale(512)[:, None]
    v = pack_weight(n((K, T)) * s, "e4m3")
    p_w2 = pack_weight(1.4 * n((512, M)) / np.sqrt(512) / u, "e2m1")
    return {
        "tab_words": v[0],
        "tab_scales": v[1],
        "w1": (n((K, 512)) / np.sqrt(K) / s * u.T).astype(np.float32),
        "w2_words": p_w2[0],
        "w2_scales": p_w2[1],
        "rT": n((M, T)).astype(np.float32),
        "offs": striped(np.random.permutation(T)[:S]),
    }


def reference(tab_words, tab_scales, w1, w2_words, w2_scales, rT, offs):
    tab_ = unpack_weight(tab_words, tab_scales, "e4m3")[:, unstriped(offs)]
    w1_ = mxq(f64(w1), 0, "e4m3")
    w2_ = unpack_weight(w2_words, w2_scales, "e2m1")
    h_ = mxq(np.maximum(w1_.T @ tab_, 0.0), 0, "e4m3")
    y = w2_.T @ h_
    return (y) + f64(rT)[:, unstriped(offs)]

@@ -1,0 +1,182 @@
+from contextlib import ExitStack
+
+import concourse.mybir as mybir
+
+K, H, M, T, S = 1536, 512, 512, 2048, 1024
+FLOPS = 2 * K * H * S + 2 * H * M * S
+
+F32 = mybir.dt.float32
+BF16 = mybir.dt.bfloat16
+I32 = mybir.dt.int32
+U32 = mybir.dt.uint32
+U16 = mybir.dt.uint16
+U8 = mybir.dt.uint8
+FP8X4 = mybir.dt.float8_e4m3fn_x4
+FP4X4 = mybir.dt.float4_e2m1fn_x4
+RELU = mybir.ActivationFunctionType.Relu
+ADD = mybir.AluOpType.add
+
+P = 128
+PACK = 4
+PASSES = K // (P * PACK)
+CHUNK = 128
+HALF = 512
+BLOCKS = M // P
+
+
+def tile_list_tabres_none_kernel(tc, tab_words, tab_scales, w1, w2_words, w2_scales, rT, offs, out):
+    nc = tc.nc
+    with ExitStack() as ctx:
+        keep = ctx.enter_context(tc.tile_pool(name="keep", bufs=1))
+        psum = ctx.enter_context(tc.psum_pool(name="psum", bufs=4))
+
+        offsets = keep.tile([P, S // 16], U16, name="offsets")
+        words = [keep.tile([P, T], U32, name="words%d" % a, align_bytes=64) for a in range(PASSES)]
+        picked = [keep.tile([P, S], U32, name="picked%d" % a, align_bytes=64) for a in range(PASSES)]
+        planes = keep.tile([P, T], U8, name="planes", align_bytes=64)
+        picked_planes = keep.tile([P, S], U8, name="picked_planes", align_bytes=64)
+        w1_raw = [keep.tile([P, PACK, H], F32, name="w1_raw%d" % a, align_bytes=64) for a in range(PASSES)]
+        w1_bf = [keep.tile([P, PACK * H], BF16, name="w1_bf%d" % a, align_bytes=64) for a in range(PASSES)]
+        w1_codes = [keep.tile([P, H], U32, name="w1_codes%d" % a, align_bytes=64) for a in range(PASSES)]
+        w1_plane = [keep.tile([P, H], U8, name="w1_plane%d" % a, align_bytes=64) for a in range(PASSES)]
+        w2_codes = keep.tile([P, 2 * M], U8, name="w2_codes", align_bytes=64)
+        w2_plane = keep.tile([P, M], U8, name="w2_plane", align_bytes=64)
+        resid = [keep.tile([P, T], F32, name="resid%d" % n, align_bytes=64) for n in range(BLOCKS)]
+        h_bf = [keep.tile([P, 2 * CHUNK * PACK], BF16, name="h_bf%d" % q, align_bytes=64) for q in range(4)]
+        h_codes = [keep.tile([P, HALF], U32, name="h_codes%d" % u, align_bytes=64) for u in range(2)]
+        h_plane = [keep.tile([P, HALF], U8, name="h_plane%d" % u, align_bytes=64) for u in range(2)]
+
+        def listed(first, count):
+            return offsets[:, first // 16 : (first + count) // 16]
+
+        def load_w1(a):
+            nc.sync.dma_start(out=w1_raw[a][:], in_=w1[512 * a : 512 * (a + 1), :].rearrange("(p j) c -> p j c", j=PACK))
+
+        def load_words(a):
+            nc.sync.dma_start(out=words[a][:].bitcast(I32), in_=tab_words[a].rearrange("p t i -> p (t i)").bitcast(I32))
+
+        def w1_views(a, m0, m1):
+            src = w1_raw[a][:].rearrange("p j (m t) -> p m j t", t=PACK)[:, m0:m1]
+            dst = w1_bf[a][:].rearrange("p (t m j) -> p m j t", t=PACK, j=PACK)[:, m0:m1]
+            return dst, src
+
+        def quantize_w1(a):
+            nc.vector.quantize_mx(out=w1_codes[a][:].bitcast(FP8X4), scales=w1_plane[a][:], in_=w1_bf[a][:])
+
+        def gather_words(a, first, count):
+            nc.vector.tensor_copy(picked[a][:, first : first + count], words[a][:].indirect(listed(first, count)))
+
+        nc.vector.memset(planes[:].bitcast(I32), 0)
+        nc.vector.memset(w2_plane[:].bitcast(I32), 0)
+        load_w1(0)
+        nc.sync.dma_start(offsets[:], offs)
+        load_w1(1)
+        load_words(0)
+        load_w1(2)
+        load_words(1)
+        load_words(2)
+        for n in range(BLOCKS):
+            nc.sync.dma_start(out=resid[n][:], in_=rT[P * n : P * (n + 1), :])
+        for q in range(4):
+            nc.gpsimd.dma_start(
+                out=planes[32 * q : 32 * q + 4 * PASSES, :].bitcast(I32), in_=tab_scales[:, 4 * q : 4 * q + 4, :].bitcast(I32)
+            )
+        for q in range(4):
+            nc.gpsimd.dma_start(out=w2_plane[32 * q : 32 * q + 4, :].bitcast(I32), in_=w2_scales[0, 4 * q : 4 * q + 4, :].bitcast(I32))
+        nc.gpsimd.dma_start(out=w2_codes[:].bitcast(I32), in_=w2_words[0].bitcast(I32))
+
+        nc.scalar.copy(*w1_views(0, 0, P))
+        nc.vector.tensor_copy(picked_planes[:], planes[:].indirect(offsets[:]))
+        quantize_w1(0)
+        nc.scalar.copy(*w1_views(1, 0, P))
+        gather_words(0, 0, S)
+        quantize_w1(1)
+        nc.scalar.copy(*w1_views(2, 0, P // 2))
+        nc.vector.tensor_copy(*w1_views(2, P // 2, P))
+        quantize_w1(2)
+        gather_words(1, 0, S)
+        for q in range(4):
+            gather_words(2, 256 * q, 256)
+
+        def first_product(c):
+            cols = slice(CHUNK * c, CHUNK * (c + 1))
+            bank = psum.tile([P, PACK, CHUNK], F32, name="bank", tag="ring")
+            for t in range(PACK):
+                wcols = slice(P * t, P * (t + 1))
+                for a in range(PASSES):
+                    nc.tensor.matmul_mx(
+                        out=bank[:, t, :],
+                        lhsT=w1_codes[a][:, wcols].bitcast(FP8X4),
+                        lhsT_scale=w1_plane[a][:, wcols],
+                        rhs=picked[a][:, cols].bitcast(FP8X4),
+                        rhs_scale=picked_planes[4 * a : P, cols],
+                        start=(a == 0),
+                        stop=(a == PASSES - 1),
+                    )
+            dst = h_bf[c // 2][:, (c % 2) * 512 : (c % 2 + 1) * 512].rearrange("p (n t) -> p n t", t=PACK)
+            nc.scalar.activation(dst, bank[:].rearrange("p t n -> p n t"), RELU)
+
+        def quantize_h(q):
+            cols = slice(256 * (q % 2), 256 * (q % 2 + 1))
+            nc.vector.quantize_mx(out=h_codes[q // 2][:, cols].bitcast(FP8X4), scales=h_plane[q // 2][:, cols], in_=h_bf[q][:])
+
+        y = {}
+
+        def second_product(u):
+            for n in range(BLOCKS):
+                y[n, u] = psum.tile([P, HALF], F32, name="y", tag="ring" if u else "first_y")
+                nc.tensor.matmul_mx(
+                    out=y[n, u][:],
+                    lhsT=w2_codes[:, 2 * P * n : 2 * P * (n + 1)].bitcast(FP4X4),
+                    lhsT_scale=w2_plane[:, P * n : P * (n + 1)],
+                    rhs=h_codes[u][:].bitcast(FP8X4),
+                    rhs_scale=h_plane[u][:],
+                    start=True,
+                    stop=True,
+                )
+
+        got = {}
+
+        def gather_resid(n, u):
+            got[n, u] = keep.tile([P, HALF], F32, name="got%d_%d" % (n, u), align_bytes=64)
+            nc.vector.tensor_copy(got[n, u][:], resid[n][:].indirect(listed(HALF * u, HALF)))
+
+        def finish(n, u, pieces=1):
+            width = HALF // pieces
+            for k in range(pieces):
+                cols = slice(width * k, width * (k + 1))
+                res = keep.tile([P, width], F32, name="res%d_%d_%d" % (n, u, k), align_bytes=64)
+                nc.vector.tensor_tensor(res[:], y[n, u][:, cols], got[n, u][:, cols], ADD)
+                first = HALF * u + width * k
+                nc.sync.dma_start(out=out[P * n : P * (n + 1), first : first + width], in_=res[:])
+
+        first_product(0)
+        first_product(1)
+        gather_resid(0, 0)
+        first_product(2)
+        first_product(3)
+        quantize_h(0)
+        gather_resid(0, 1)
+        quantize_h(1)
+        second_product(0)
+        first_product(4)
+        first_product(5)
+        gather_resid(1, 0)
+        first_product(6)
+        first_product(7)
+        gather_resid(1, 1)
+        quantize_h(2)
+        finish(0, 0)
+        finish(1, 0)
+        quantize_h(3)
+        second_product(1)
+        gather_resid(2, 0)
+        finish(2, 0)
+        gather_resid(2, 1)
+        finish(0, 1)
+        finish(1, 1)
+        gather_resid(3, 0)
+        finish(2, 1)
+        finish(3, 0)
+        gather_resid(3, 1)
+        finish(3, 1, pieces=2)

@@ -31,18 +31,33 @@ def tile_list_tabres_none_kernel(tc, tab_words, tab_scales, w1, w2_words, w2_sca
         psum = ctx.enter_context(tc.psum_pool(name="psum", bufs=4))
 
         offsets = keep.tile([P, S // 16], U16, name="offsets")
-        words = [keep.tile([P, T], U32, name="words%d" % a, align_bytes=64) for a in range(PASSES)]
-        picked = [keep.tile([P, S], U32, name="picked%d" % a, align_bytes=64) for a in range(PASSES)]
+        def shared(tag, shape, dtype):
+            return keep.tile(shape, dtype, name=tag, tag=tag, align_bytes=64)
+
+        words, w1_raw, w1_bf, resid, picked = {}, {}, {}, {}, {}
+        w1_raw[0] = shared("slot0", [P, PACK, H], F32)
+        w1_raw[1] = shared("slot1", [P, PACK, H], F32)
+        for a in range(PASSES):
+            for v in range(2):
+                w1_bf[a, v] = shared("cast%d%d" % (a, v), [P, PACK * H // 2], BF16)
+        w1_raw[2] = shared("cast00", [P, PACK, H], F32)
+        words[0] = shared("cast01", [P, T], U32)
+        picked_planes = shared("cast10", [P, S], U8)
+        words[1] = shared("slot1", [P, T], U32)
+        words[2] = shared("cast11", [P, T], U32)
+        resid[0] = shared("cast20", [P, T], F32)
+        picked[0] = shared("cast00", [P, S], U32)
+        picked[1] = shared("cast21", [P, S], U32)
+        picked[2] = shared("picked2", [P, S], U32)
+        resid[1] = shared("cast01", [P, T], F32)
+        resid[2] = shared("slot1", [P, T], F32)
+        resid[3] = shared("cast11", [P, T], F32)
+        w2_plane = keep.tile([P, M], U8, name="w2_plane", align_bytes=64)
         planes = keep.tile([P, T], U8, name="planes", align_bytes=64)
-        picked_planes = keep.tile([P, S], U8, name="picked_planes", align_bytes=64)
-        w1_raw = [keep.tile([P, PACK, H], F32, name="w1_raw%d" % a, align_bytes=64) for a in range(PASSES)]
-        w1_bf = [keep.tile([P, PACK * H], BF16, name="w1_bf%d" % a, align_bytes=64) for a in range(PASSES)]
         w1_codes = [keep.tile([P, H], U32, name="w1_codes%d" % a, align_bytes=64) for a in range(PASSES)]
         w1_plane = [keep.tile([P, H], U8, name="w1_plane%d" % a, align_bytes=64) for a in range(PASSES)]
         w2_codes = keep.tile([P, 2 * M], U8, name="w2_codes", align_bytes=64)
-        w2_plane = keep.tile([P, M], U8, name="w2_plane", align_bytes=64)
-        resid = [keep.tile([P, T], F32, name="resid%d" % n, align_bytes=64) for n in range(BLOCKS)]
-        h_bf = [keep.tile([P, 2 * CHUNK * PACK], BF16, name="h_bf%d" % q, align_bytes=64) for q in range(4)]
+        h_bf = [shared("h_bf%d" % u, [P, HALF * PACK], BF16) for u in range(2)]
         h_codes = [keep.tile([P, HALF], U32, name="h_codes%d" % u, align_bytes=64) for u in range(2)]
         h_plane = [keep.tile([P, HALF], U8, name="h_plane%d" % u, align_bytes=64) for u in range(2)]
 
@@ -55,48 +70,59 @@ def tile_list_tabres_none_kernel(tc, tab_words, tab_scales, w1, w2_words, w2_sca
         def load_words(a):
             nc.sync.dma_start(out=words[a][:].bitcast(I32), in_=tab_words[a].rearrange("p t i -> p (t i)").bitcast(I32))
 
-        def w1_views(a, m0, m1):
-            src = w1_raw[a][:].rearrange("p j (m t) -> p m j t", t=PACK)[:, m0:m1]
-            dst = w1_bf[a][:].rearrange("p (t m j) -> p m j t", t=PACK, j=PACK)[:, m0:m1]
+        def w1_views(a, v):
+            src = w1_raw[a][:].rearrange("p j (m t) -> p m t j", t=PACK)[:, :, 2 * v : 2 * v + 2, :]
+            dst = w1_bf[a, v][:].rearrange("p (t m j) -> p m t j", t=2, j=PACK)
             return dst, src
 
-        def quantize_w1(a):
-            nc.vector.quantize_mx(out=w1_codes[a][:].bitcast(FP8X4), scales=w1_plane[a][:], in_=w1_bf[a][:])
+        def quantize_w1(a, v):
+            cols = slice(256 * v, 256 * (v + 1))
+            nc.vector.quantize_mx(out=w1_codes[a][:, cols].bitcast(FP8X4), scales=w1_plane[a][:, cols], in_=w1_bf[a, v][:])
 
         def gather_words(a, first, count):
             nc.vector.tensor_copy(picked[a][:, first : first + count], words[a][:].indirect(listed(first, count)))
 
-        nc.vector.memset(planes[:].bitcast(I32), 0)
-        nc.vector.memset(w2_plane[:].bitcast(I32), 0)
-        load_w1(0)
-        nc.sync.dma_start(offsets[:], offs)
-        load_w1(1)
-        load_words(0)
-        load_w1(2)
-        load_words(1)
-        load_words(2)
-        for n in range(BLOCKS):
+        def load_resid(n):
             nc.sync.dma_start(out=resid[n][:], in_=rT[P * n : P * (n + 1), :])
+
+        nc.vector.memset(planes[:].bitcast(I32), 0)
+        nc.gpsimd.memset(w2_plane[:].bitcast(I32), 0)
+        nc.sync.dma_start(offsets[:], offs)
+        load_w1(0)
+        load_w1(1)
+        nc.sync.dma_start(out=w2_codes[:].bitcast(I32), in_=w2_words[0].bitcast(I32))
         for q in range(4):
-            nc.gpsimd.dma_start(
+            nc.sync.dma_start(
                 out=planes[32 * q : 32 * q + 4 * PASSES, :].bitcast(I32), in_=tab_scales[:, 4 * q : 4 * q + 4, :].bitcast(I32)
             )
         for q in range(4):
             nc.gpsimd.dma_start(out=w2_plane[32 * q : 32 * q + 4, :].bitcast(I32), in_=w2_scales[0, 4 * q : 4 * q + 4, :].bitcast(I32))
-        nc.gpsimd.dma_start(out=w2_codes[:].bitcast(I32), in_=w2_words[0].bitcast(I32))
-
-        nc.scalar.copy(*w1_views(0, 0, P))
+        nc.vector.tensor_copy(*w1_views(0, 0))
+        nc.scalar.copy(*w1_views(0, 1))
+        quantize_w1(0, 0)
+        load_w1(2)
+        quantize_w1(0, 1)
+        load_words(0)
+        nc.vector.tensor_copy(*w1_views(1, 0))
+        nc.scalar.copy(*w1_views(1, 1))
+        load_words(1)
+        quantize_w1(1, 0)
         nc.vector.tensor_copy(picked_planes[:], planes[:].indirect(offsets[:]))
-        quantize_w1(0)
-        nc.scalar.copy(*w1_views(1, 0, P))
+        quantize_w1(1, 1)
+        load_words(2)
+        nc.vector.tensor_copy(*w1_views(2, 0))
+        nc.scalar.copy(*w1_views(2, 1))
+        quantize_w1(2, 0)
+        load_resid(0)
+        quantize_w1(2, 1)
         gather_words(0, 0, S)
-        quantize_w1(1)
-        nc.scalar.copy(*w1_views(2, 0, P // 2))
-        nc.vector.tensor_copy(*w1_views(2, P // 2, P))
-        quantize_w1(2)
+        load_resid(1)
         gather_words(1, 0, S)
-        for q in range(4):
-            gather_words(2, 256 * q, 256)
+        load_resid(2)
+        gather_words(2, 0, 256)
+        gather_words(2, 256, 256)
+        gather_words(2, 512, 512)
+        load_resid(3)
 
         def first_product(c):
             cols = slice(CHUNK * c, CHUNK * (c + 1))
@@ -113,12 +139,11 @@ def tile_list_tabres_none_kernel(tc, tab_words, tab_scales, w1, w2_words, w2_sca
                         start=(a == 0),
                         stop=(a == PASSES - 1),
                     )
-            dst = h_bf[c // 2][:, (c % 2) * 512 : (c % 2 + 1) * 512].rearrange("p (n t) -> p n t", t=PACK)
+            dst = h_bf[c // 4][:, (c % 4) * 512 : (c % 4 + 1) * 512].rearrange("p (n t) -> p n t", t=PACK)
             nc.scalar.activation(dst, bank[:].rearrange("p t n -> p n t"), RELU)
 
-        def quantize_h(q):
-            cols = slice(256 * (q % 2), 256 * (q % 2 + 1))
-            nc.vector.quantize_mx(out=h_codes[q // 2][:, cols].bitcast(FP8X4), scales=h_plane[q // 2][:, cols], in_=h_bf[q][:])
+        def quantize_h(u):
+            nc.vector.quantize_mx(out=h_codes[u][:].bitcast(FP8X4), scales=h_plane[u][:], in_=h_bf[u][:])
 
         y = {}
 
@@ -136,47 +161,52 @@ def tile_list_tabres_none_kernel(tc, tab_words, tab_scales, w1, w2_words, w2_sca
                 )
 
         got = {}
+        for n in range(BLOCKS - 1):
+            whole = shared("got%d" % n, [P, S], F32)
+            got[n, 0], got[n, 1], got[n] = whole[:, 0:HALF], whole[:, HALF:S], whole[:]
+        got[3, 0] = shared("got3", [P, HALF], F32)[:]
+        got[3, 1] = shared("h_bf1", [P, HALF], F32)[:]
 
-        def gather_resid(n, u):
-            got[n, u] = keep.tile([P, HALF], F32, name="got%d_%d" % (n, u), align_bytes=64)
-            nc.vector.tensor_copy(got[n, u][:], resid[n][:].indirect(listed(HALF * u, HALF)))
+        def gather_resid(n):
+            nc.vector.tensor_copy(got[n], resid[n][:].indirect(offsets[:]))
+
+        def gather_resid_half(n, u):
+            nc.vector.tensor_copy(got[n, u], resid[n][:].indirect(listed(HALF * u, HALF)))
 
         def finish(n, u, pieces=1):
             width = HALF // pieces
             for k in range(pieces):
                 cols = slice(width * k, width * (k + 1))
                 res = keep.tile([P, width], F32, name="res%d_%d_%d" % (n, u, k), align_bytes=64)
-                nc.vector.tensor_tensor(res[:], y[n, u][:, cols], got[n, u][:, cols], ADD)
                 first = HALF * u + width * k
+                nc.vector.tensor_tensor(res[:], y[n, u][:, cols], got[n, u][:, cols], ADD)
                 nc.sync.dma_start(out=out[P * n : P * (n + 1), first : first + width], in_=res[:])
 
-        first_product(0)
-        first_product(1)
-        gather_resid(0, 0)
-        first_product(2)
-        first_product(3)
+        def finish_on_gpsimd(n, u):
+            staged = shared("staged%d" % n, [P, HALF], F32)
+            nc.scalar.copy(staged[:], y[n, u][:])
+            res = shared("sum%d" % n, [P, HALF], F32)
+            nc.gpsimd.tensor_tensor(res[:], staged[:], got[n, u], ADD)
+            nc.sync.dma_start(out=out[P * n : P * (n + 1), HALF * u : HALF * (u + 1)], in_=res[:])
+
+        for c in range(4):
+            first_product(c)
+        gather_resid(0)
+        gather_resid(1)
         quantize_h(0)
-        gather_resid(0, 1)
-        quantize_h(1)
-        second_product(0)
         first_product(4)
         first_product(5)
-        gather_resid(1, 0)
+        second_product(0)
         first_product(6)
         first_product(7)
-        gather_resid(1, 1)
-        quantize_h(2)
-        finish(0, 0)
-        finish(1, 0)
-        quantize_h(3)
+        gather_resid(2)
+        gather_resid_half(3, 0)
+        quantize_h(1)
         second_product(1)
-        gather_resid(2, 0)
-        finish(2, 0)
-        gather_resid(2, 1)
+        for n in range(BLOCKS):
+            finish_on_gpsimd(n, 0)
+        gather_resid_half(3, 1)
         finish(0, 1)
         finish(1, 1)
-        gather_resid(3, 0)
         finish(2, 1)
-        finish(3, 0)
-        gather_resid(3, 1)
         finish(3, 1, pieces=2)

@@ -22,134 +22,133 @@ PASSES = K // (P * PACK)
 CHUNK = 128
 HALF = 512
 BLOCKS = M // P
+SLOT = 10240
 
 
 def tile_list_tabres_none_kernel(tc, tab_words, tab_scales, w1, w2_words, w2_scales, rT, offs, out):
     nc = tc.nc
     with ExitStack() as ctx:
         keep = ctx.enter_context(tc.tile_pool(name="keep", bufs=1))
-        psum = ctx.enter_context(tc.psum_pool(name="psum", bufs=4))
+        psum = ctx.enter_context(tc.psum_pool(name="psum", bufs=1))
+
+        arena = ctx.enter_context(tc.tile_pool(name="arena", bufs=1))
 
         offsets = keep.tile([P, S // 16], U16, name="offsets")
+
+        def placed(name, shape, dtype, at):
+            return arena.tile(shape, dtype, name=name, tag=name, align_bytes=64, offset=at)
+
         def shared(tag, shape, dtype):
             return keep.tile(shape, dtype, name=tag, tag=tag, align_bytes=64)
-
-        words, w1_raw, w1_bf, resid, picked = {}, {}, {}, {}, {}
-        w1_raw[0] = shared("slot0", [P, PACK, H], F32)
-        w1_raw[1] = shared("slot1", [P, PACK, H], F32)
-        for a in range(PASSES):
-            for v in range(2):
-                w1_bf[a, v] = shared("cast%d%d" % (a, v), [P, PACK * H // 2], BF16)
-        w1_raw[2] = shared("cast00", [P, PACK, H], F32)
-        words[0] = shared("cast01", [P, T], U32)
-        picked_planes = shared("cast10", [P, S], U8)
-        words[1] = shared("slot1", [P, T], U32)
-        words[2] = shared("cast11", [P, T], U32)
-        resid[0] = shared("cast20", [P, T], F32)
-        picked[0] = shared("cast00", [P, S], U32)
-        picked[1] = shared("cast21", [P, S], U32)
-        picked[2] = shared("picked2", [P, S], U32)
-        resid[1] = shared("cast01", [P, T], F32)
-        resid[2] = shared("slot1", [P, T], F32)
-        resid[3] = shared("cast11", [P, T], F32)
-        w2_plane = keep.tile([P, M], U8, name="w2_plane", align_bytes=64)
-        planes = keep.tile([P, T], U8, name="planes", align_bytes=64)
-        w1_codes = [keep.tile([P, H], U32, name="w1_codes%d" % a, align_bytes=64) for a in range(PASSES)]
-        w1_plane = [keep.tile([P, H], U8, name="w1_plane%d" % a, align_bytes=64) for a in range(PASSES)]
-        w2_codes = keep.tile([P, 2 * M], U8, name="w2_codes", align_bytes=64)
-        h_bf = [shared("h_bf%d" % u, [P, HALF * PACK], BF16) for u in range(2)]
-        h_codes = [keep.tile([P, HALF], U32, name="h_codes%d" % u, align_bytes=64) for u in range(2)]
-        h_plane = [keep.tile([P, HALF], U8, name="h_plane%d" % u, align_bytes=64) for u in range(2)]
 
         def listed(first, count):
             return offsets[:, first // 16 : (first + count) // 16]
 
-        def load_w1(a):
-            nc.sync.dma_start(out=w1_raw[a][:], in_=w1[512 * a : 512 * (a + 1), :].rearrange("(p j) c -> p j c", j=PACK))
+        def load_big(name, at, shape, dtype, src):
+            tile = placed(name, shape, dtype, at)
+            nc.sync.dma_start(out=tile[:].bitcast(I32) if dtype == U32 else tile[:], in_=src)
+            return tile
 
-        def load_words(a):
-            nc.sync.dma_start(out=words[a][:].bitcast(I32), in_=tab_words[a].rearrange("p t i -> p (t i)").bitcast(I32))
+        def load_w1(a, at):
+            return load_big("w1_raw%d" % a, at, [P, PACK, H], F32, w1[512 * a : 512 * (a + 1), :].rearrange("(p j) c -> p j c", j=PACK))
 
-        def w1_views(a, v):
-            src = w1_raw[a][:].rearrange("p j (m t) -> p m t j", t=PACK)[:, :, 2 * v : 2 * v + 2, :]
-            dst = w1_bf[a, v][:].rearrange("p (t m j) -> p m t j", t=2, j=PACK)
-            return dst, src
+        def load_words(a, at):
+            return load_big("words%d" % a, at, [P, T], U32, tab_words[a].rearrange("p t i -> p (t i)").bitcast(I32))
 
-        def quantize_w1(a, v):
-            cols = slice(256 * v, 256 * (v + 1))
-            nc.vector.quantize_mx(out=w1_codes[a][:, cols].bitcast(FP8X4), scales=w1_plane[a][:, cols], in_=w1_bf[a, v][:])
+        def load_resid(n, at):
+            return load_big("resid%d" % n, at, [P, T], F32, rT[P * n : P * (n + 1), :])
 
-        def gather_words(a, first, count):
-            nc.vector.tensor_copy(picked[a][:, first : first + count], words[a][:].indirect(listed(first, count)))
+        planes = placed("planes", [P, T], U8, 3 * SLOT)
+        w2_plane = shared("w2_plane", [P, M], U8)
+        picked = {}
+        w1_codes = [shared("w1_codes%d" % a, [P, H], U32) for a in range(PASSES)]
+        w1_plane = [shared("w1_plane%d" % a, [P, H], U8) for a in range(PASSES)]
+        h_bf = [shared("h_bf%d" % u, [P, HALF * PACK], BF16) for u in range(2)]
+        h_codes = [shared("h_codes%d" % u, [P, HALF], U32) for u in range(2)]
+        h_plane = [shared("h_plane%d" % u, [P, HALF], U8) for u in range(2)]
+        banks = [psum.tile([P, PACK, CHUNK], F32, name="bank%d" % c, tag="bank%d" % c) for c in range(S // CHUNK)]
 
-        def load_resid(n):
-            nc.sync.dma_start(out=resid[n][:], in_=rT[P * n : P * (n + 1), :])
+        def prepare_w1(a, raw, copies):
+            halves = []
+            for v, copy in enumerate(copies):
+                bf = shared("w1_bf%d_%d" % (a, v), [P, PACK * H // 2], BF16)
+                src = raw[:].rearrange("p j (m t) -> p m t j", t=PACK)[:, :, 2 * v : 2 * v + 2, :]
+                copy(bf[:].rearrange("p (t m j) -> p m t j", t=2, j=PACK), src)
+                halves.append(bf)
+            for v, bf in enumerate(halves):
+                cols = slice(256 * v, 256 * (v + 1))
+                nc.vector.quantize_mx(out=w1_codes[a][:, cols].bitcast(FP8X4), scales=w1_plane[a][:, cols], in_=bf[:])
+
+        def first_product(a, c):
+            cols = slice(CHUNK * c, CHUNK * (c + 1))
+            for t in range(PACK):
+                wcols = slice(P * t, P * (t + 1))
+                nc.tensor.matmul_mx(
+                    out=banks[c][:, t, :],
+                    lhsT=w1_codes[a][:, wcols].bitcast(FP8X4),
+                    lhsT_scale=w1_plane[a][:, wcols],
+                    rhs=picked[a][:, cols].bitcast(FP8X4),
+                    rhs_scale=picked_planes[4 * a : P, cols],
+                    start=(a == 0 and t == 0),
+                    stop=(a == PASSES - 1 and t == PACK - 1),
+                )
+
+        def relu(c):
+            dst = h_bf[c // 4][:, (c % 4) * 512 : (c % 4 + 1) * 512].rearrange("p (n t) -> p n t", t=PACK)
+            nc.scalar.activation(dst, banks[c][:].rearrange("p t n -> p n t"), RELU)
+
+        def gather_words(a, words, first, count):
+            nc.vector.tensor_copy(picked[a][:, first : first + count], words[:].indirect(listed(first, count)))
+
+        def gather_and_multiply(a, words, counts):
+            first = 0
+            for count in counts:
+                gather_words(a, words, first, count)
+                for c in range(first // CHUNK, (first + count) // CHUNK):
+                    first_product(a, c)
+                    if a == PASSES - 1:
+                        relu(c)
+                first = first + count
 
         nc.vector.memset(planes[:].bitcast(I32), 0)
         nc.gpsimd.memset(w2_plane[:].bitcast(I32), 0)
         nc.sync.dma_start(offsets[:], offs)
-        load_w1(0)
-        load_w1(1)
-        nc.sync.dma_start(out=w2_codes[:].bitcast(I32), in_=w2_words[0].bitcast(I32))
+        words = load_words(0, SLOT)
+        raw = load_w1(0, 4 * SLOT)
         for q in range(4):
             nc.sync.dma_start(
                 out=planes[32 * q : 32 * q + 4 * PASSES, :].bitcast(I32), in_=tab_scales[:, 4 * q : 4 * q + 4, :].bitcast(I32)
             )
         for q in range(4):
             nc.gpsimd.dma_start(out=w2_plane[32 * q : 32 * q + 4, :].bitcast(I32), in_=w2_scales[0, 4 * q : 4 * q + 4, :].bitcast(I32))
-        nc.vector.tensor_copy(*w1_views(0, 0))
-        nc.scalar.copy(*w1_views(0, 1))
-        quantize_w1(0, 0)
-        load_w1(2)
-        quantize_w1(0, 1)
-        load_words(0)
-        nc.vector.tensor_copy(*w1_views(1, 0))
-        nc.scalar.copy(*w1_views(1, 1))
-        load_words(1)
-        quantize_w1(1, 0)
+        picked[0] = shared("picked0", [P, S], U32)
+        gather_words(0, words, 0, S)
+        prepare_w1(0, raw, (nc.vector.tensor_copy, nc.scalar.copy))
+        picked_planes = shared("w1_bf0_0", [P, S], U8)
         nc.vector.tensor_copy(picked_planes[:], planes[:].indirect(offsets[:]))
-        quantize_w1(1, 1)
-        load_words(2)
-        nc.vector.tensor_copy(*w1_views(2, 0))
-        nc.scalar.copy(*w1_views(2, 1))
-        quantize_w1(2, 0)
-        load_resid(0)
-        quantize_w1(2, 1)
-        gather_words(0, 0, S)
-        load_resid(1)
-        gather_words(1, 0, S)
-        load_resid(2)
-        gather_words(2, 0, 256)
-        gather_words(2, 256, 256)
-        gather_words(2, 512, 512)
-        load_resid(3)
+        for c in range(S // CHUNK):
+            first_product(0, c)
+        words = load_words(1, 6 * SLOT)
+        raw = load_w1(1, SLOT - 7168)
+        picked[1] = placed("picked1", [P, S], U32, 3 * SLOT - 3072)
+        gather_words(1, words, 0, HALF)
+        gather_words(1, words, HALF, HALF)
+        prepare_w1(1, raw, (nc.vector.tensor_copy, nc.scalar.copy))
+        for c in range(S // CHUNK):
+            first_product(1, c)
+        prepare_w1(2, load_w1(2, SLOT + 7168), (nc.vector.tensor_copy, nc.scalar.copy))
+        picked[2] = shared("picked2", [P, S], U32)
+        gather_and_multiply(2, load_words(2, 3 * SLOT + 1024), (256, 256, 512))
+        w2_codes = shared("w1_bf0_1", [P, 2 * M], U8)
+        nc.sync.dma_start(out=w2_codes[:].bitcast(I32), in_=w2_words[0].bitcast(I32))
+        resid = [load_resid(n, at) for n, at in enumerate((4 * SLOT, 6 * SLOT - 7168, 6 * SLOT + 7168, SLOT - 7168))]
 
-        def first_product(c):
-            cols = slice(CHUNK * c, CHUNK * (c + 1))
-            bank = psum.tile([P, PACK, CHUNK], F32, name="bank", tag="ring")
-            for t in range(PACK):
-                wcols = slice(P * t, P * (t + 1))
-                for a in range(PASSES):
-                    nc.tensor.matmul_mx(
-                        out=bank[:, t, :],
-                        lhsT=w1_codes[a][:, wcols].bitcast(FP8X4),
-                        lhsT_scale=w1_plane[a][:, wcols],
-                        rhs=picked[a][:, cols].bitcast(FP8X4),
-                        rhs_scale=picked_planes[4 * a : P, cols],
-                        start=(a == 0),
-                        stop=(a == PASSES - 1),
-                    )
-            dst = h_bf[c // 4][:, (c % 4) * 512 : (c % 4 + 1) * 512].rearrange("p (n t) -> p n t", t=PACK)
-            nc.scalar.activation(dst, bank[:].rearrange("p t n -> p n t"), RELU)
-
-        def quantize_h(u):
-            nc.vector.quantize_mx(out=h_codes[u][:].bitcast(FP8X4), scales=h_plane[u][:], in_=h_bf[u][:])
-
-        y = {}
+        y, got = {}, {}
 
         def second_product(u):
+            nc.vector.quantize_mx(out=h_codes[u][:].bitcast(FP8X4), scales=h_plane[u][:], in_=h_bf[u][:])
             for n in range(BLOCKS):
-                y[n, u] = psum.tile([P, HALF], F32, name="y", tag="ring" if u else "first_y")
+                y[n, u] = psum.tile([P, HALF], F32, name="y%d_%d" % (n, u), tag="bank%d" % (4 * u + n))
                 nc.tensor.matmul_mx(
                     out=y[n, u][:],
                     lhsT=w2_codes[:, 2 * P * n : 2 * P * (n + 1)].bitcast(FP4X4),
@@ -160,53 +159,35 @@ def tile_list_tabres_none_kernel(tc, tab_words, tab_scales, w1, w2_words, w2_sca
                     stop=True,
                 )
 
-        got = {}
-        for n in range(BLOCKS - 1):
-            whole = shared("got%d" % n, [P, S], F32)
-            got[n, 0], got[n, 1], got[n] = whole[:, 0:HALF], whole[:, HALF:S], whole[:]
-        got[3, 0] = shared("got3", [P, HALF], F32)[:]
-        got[3, 1] = shared("h_bf1", [P, HALF], F32)[:]
+        def gather_resid(n, u, tag):
+            got[n, u] = shared(tag, [P, HALF], F32)
+            nc.vector.tensor_copy(got[n, u][:], resid[n][:].indirect(listed(HALF * u, HALF)))
 
-        def gather_resid(n):
-            nc.vector.tensor_copy(got[n], resid[n][:].indirect(offsets[:]))
-
-        def gather_resid_half(n, u):
-            nc.vector.tensor_copy(got[n, u], resid[n][:].indirect(listed(HALF * u, HALF)))
-
-        def finish(n, u, pieces=1):
-            width = HALF // pieces
-            for k in range(pieces):
-                cols = slice(width * k, width * (k + 1))
-                res = keep.tile([P, width], F32, name="res%d_%d_%d" % (n, u, k), align_bytes=64)
-                first = HALF * u + width * k
-                nc.vector.tensor_tensor(res[:], y[n, u][:, cols], got[n, u][:, cols], ADD)
-                nc.sync.dma_start(out=out[P * n : P * (n + 1), first : first + width], in_=res[:])
-
-        def finish_on_gpsimd(n, u):
-            staged = shared("staged%d" % n, [P, HALF], F32)
-            nc.scalar.copy(staged[:], y[n, u][:])
-            res = shared("sum%d" % n, [P, HALF], F32)
-            nc.gpsimd.tensor_tensor(res[:], staged[:], got[n, u], ADD)
+        def store(n, u, res):
             nc.sync.dma_start(out=out[P * n : P * (n + 1), HALF * u : HALF * (u + 1)], in_=res[:])
 
-        for c in range(4):
-            first_product(c)
-        gather_resid(0)
-        gather_resid(1)
-        quantize_h(0)
-        first_product(4)
-        first_product(5)
+        def finish_on_vector(n, u):
+            res = shared("res%d_%d" % (n, u), [P, HALF], F32)
+            nc.vector.tensor_tensor(res[:], y[n, u][:], got[n, u][:], ADD)
+            store(n, u, res)
+
+        def finish_on_gpsimd(n, u):
+            staged = shared("staged%d_%d" % (n, u), [P, HALF], F32)
+            nc.scalar.copy(staged[:], y[n, u][:])
+            res = shared("res%d_%d" % (n, u), [P, HALF], F32)
+            nc.gpsimd.tensor_tensor(res[:], staged[:], got[n, u][:], ADD)
+            store(n, u, res)
+
+        gather_resid(0, 0, "got00")
         second_product(0)
-        first_product(6)
-        first_product(7)
-        gather_resid(2)
-        gather_resid_half(3, 0)
-        quantize_h(1)
+        gather_resid(0, 1, "h_bf0")
+        gather_resid(1, 0, "got10")
         second_product(1)
-        for n in range(BLOCKS):
-            finish_on_gpsimd(n, 0)
-        gather_resid_half(3, 1)
-        finish(0, 1)
-        finish(1, 1)
-        finish(2, 1)
-        finish(3, 1, pieces=2)
+        gather_resid(1, 1, "h_bf1")
+        for n in (2, 3):
+            for u in range(2):
+                gather_resid(n, u, "got%d%d" % (n, u))
+        for n, u in ((0, 0), (1, 0), (0, 1), (1, 1), (2, 0), (2, 1)):
+            finish_on_gpsimd(n, u)
+        finish_on_vector(3, 0)
+        finish_on_vector(3, 1)

@@ -171,23 +171,22 @@ def tile_list_tabres_none_kernel(tc, tab_words, tab_scales, w1, w2_words, w2_sca
             nc.vector.tensor_tensor(res[:], y[n, u][:], got[n, u][:], ADD)
             store(n, u, res)
 
-        def finish_on_gpsimd(n, u):
+        def finish_fused(n, u):
             staged = shared("staged%d_%d" % (n, u), [P, HALF], F32)
             nc.scalar.copy(staged[:], y[n, u][:])
             res = shared("res%d_%d" % (n, u), [P, HALF], F32)
-            nc.gpsimd.tensor_tensor(res[:], staged[:], got[n, u][:], ADD)
+            nc.vector.tensor_tensor(res[:], resid[n][:].indirect(listed(HALF * u, HALF)), staged[:], ADD)
             store(n, u, res)
 
         gather_resid(0, 0, "got00")
         second_product(0)
         gather_resid(0, 1, "h_bf0")
-        gather_resid(1, 0, "got10")
+        finish_on_vector(0, 0)
         second_product(1)
-        gather_resid(1, 1, "h_bf1")
-        for n in (2, 3):
-            for u in range(2):
-                gather_resid(n, u, "got%d%d" % (n, u))
-        for n, u in ((0, 0), (1, 0), (0, 1), (1, 1), (2, 0), (2, 1)):
-            finish_on_gpsimd(n, u)
-        finish_on_vector(3, 0)
-        finish_on_vector(3, 1)
+        finish_fused(1, 0)
+        finish_fused(2, 0)
+        finish_on_vector(0, 1)
+        finish_fused(1, 1)
+        finish_fused(2, 1)
+        finish_fused(3, 0)
+        finish_fused(3, 1)

@@ -123,14 +123,14 @@ def tile_list_tabres_none_kernel(tc, tab_words, tab_scales, w1, w2_words, w2_sca
             nc.gpsimd.dma_start(out=w2_plane[32 * q : 32 * q + 4, :].bitcast(I32), in_=w2_scales[0, 4 * q : 4 * q + 4, :].bitcast(I32))
         picked[0] = shared("picked0", [P, S], U32)
         gather_words(0, words, 0, S)
-        prepare_w1(0, raw, (nc.vector.tensor_copy, nc.scalar.copy))
-        picked_planes = shared("w1_bf0_0", [P, S], U8)
+        picked_planes = placed("picked_planes", [P, S], U8, SLOT + 2048)
         nc.vector.tensor_copy(picked_planes[:], planes[:].indirect(offsets[:]))
+        prepare_w1(0, raw, (nc.scalar.copy, nc.scalar.copy))
         for c in range(S // CHUNK):
             first_product(0, c)
         words = load_words(1, 6 * SLOT)
         raw = load_w1(1, SLOT - 7168)
-        picked[1] = placed("picked1", [P, S], U32, 3 * SLOT - 3072)
+        picked[1] = shared("w1_bf0_0", [P, S], U32)
         gather_words(1, words, 0, HALF)
         gather_words(1, words, HALF, HALF)
         prepare_w1(1, raw, (nc.vector.tensor_copy, nc.scalar.copy))
@@ -139,9 +139,10 @@ def tile_list_tabres_none_kernel(tc, tab_words, tab_scales, w1, w2_words, w2_sca
         prepare_w1(2, load_w1(2, SLOT + 7168), (nc.vector.tensor_copy, nc.scalar.copy))
         picked[2] = shared("picked2", [P, S], U32)
         gather_and_multiply(2, load_words(2, 3 * SLOT + 1024), (256, 256, 512))
+        resid = [load_resid(0, 4 * SLOT)]
         w2_codes = shared("w1_bf0_1", [P, 2 * M], U8)
         nc.sync.dma_start(out=w2_codes[:].bitcast(I32), in_=w2_words[0].bitcast(I32))
-        resid = [load_resid(n, at) for n, at in enumerate((4 * SLOT, 6 * SLOT - 7168, 6 * SLOT + 7168, SLOT - 7168))]
+        resid = resid + [load_resid(n + 1, at) for n, at in enumerate((6 * SLOT - 7168, 6 * SLOT + 7168, SLOT - 7168))]
 
         y, got = {}, {}
 
@@ -163,20 +164,24 @@ def tile_list_tabres_none_kernel(tc, tab_words, tab_scales, w1, w2_words, w2_sca
             got[n, u] = shared(tag, [P, HALF], F32)
             nc.vector.tensor_copy(got[n, u][:], resid[n][:].indirect(listed(HALF * u, HALF)))
 
-        def store(n, u, res):
-            nc.sync.dma_start(out=out[P * n : P * (n + 1), HALF * u : HALF * (u + 1)], in_=res[:])
+        def store(n, first, count, res):
+            nc.sync.dma_start(out=out[P * n : P * (n + 1), first : first + count], in_=res[:])
 
         def finish_on_vector(n, u):
             res = shared("res%d_%d" % (n, u), [P, HALF], F32)
             nc.vector.tensor_tensor(res[:], y[n, u][:], got[n, u][:], ADD)
-            store(n, u, res)
+            store(n, HALF * u, HALF, res)
 
-        def finish_fused(n, u):
+        def finish_fused(n, u, counts=(HALF,)):
             staged = shared("staged%d_%d" % (n, u), [P, HALF], F32)
             nc.scalar.copy(staged[:], y[n, u][:])
-            res = shared("res%d_%d" % (n, u), [P, HALF], F32)
-            nc.vector.tensor_tensor(res[:], resid[n][:].indirect(listed(HALF * u, HALF)), staged[:], ADD)
-            store(n, u, res)
+            done = 0
+            for count in counts:
+                res = shared("res%d_%d_%d" % (n, u, done), [P, count], F32)
+                first = HALF * u + done
+                nc.vector.tensor_tensor(res[:], resid[n][:].indirect(listed(first, count)), staged[:, done : done + count], ADD)
+                store(n, first, count, res)
+                done = done + count
 
         gather_resid(0, 0, "got00")
         second_product(0)
@@ -189,4 +194,4 @@ def tile_list_tabres_none_kernel(tc, tab_words, tab_scales, w1, w2_words, w2_sca
         finish_fused(1, 1)
         finish_fused(2, 1)
         finish_fused(3, 0)
-        finish_fused(3, 1)
+        finish_fused(3, 1, (256, 128, 128))

@@ -110,15 +110,15 @@ def tile_list_tabres_none_kernel(tc, tab_words, tab_scales, w1, w2_words, w2_sca
                         relu(c)
                 first = first + count
 
-        nc.vector.memset(planes[:].bitcast(I32), 0)
+        nc.gpsimd.memset(planes[:].bitcast(I32), 0)
         nc.gpsimd.memset(w2_plane[:].bitcast(I32), 0)
-        nc.sync.dma_start(offsets[:], offs)
         words = load_words(0, SLOT)
-        raw = load_w1(0, 4 * SLOT)
+        nc.sync.dma_start(offsets[:], offs)
         for q in range(4):
-            nc.sync.dma_start(
+            (nc.sync if q % 2 else nc.scalar).dma_start(
                 out=planes[32 * q : 32 * q + 4 * PASSES, :].bitcast(I32), in_=tab_scales[:, 4 * q : 4 * q + 4, :].bitcast(I32)
             )
+        raw = load_w1(0, 4 * SLOT)
         for q in range(4):
             nc.gpsimd.dma_start(out=w2_plane[32 * q : 32 * q + 4, :].bitcast(I32), in_=w2_scales[0, 4 * q : 4 * q + 4, :].bitcast(I32))
         picked[0] = shared("picked0", [P, S], U32)
@@ -194,4 +194,4 @@ def tile_list_tabres_none_kernel(tc, tab_words, tab_scales, w1, w2_words, w2_sca
         finish_fused(1, 1)
         finish_fused(2, 1)
         finish_fused(3, 0)
-        finish_fused(3, 1, (256, 128, 128))
+        finish_fused(3, 1, (256, 256))

@@ -110,8 +110,8 @@ def tile_list_tabres_none_kernel(tc, tab_words, tab_scales, w1, w2_words, w2_sca
                         relu(c)
                 first = first + count
 
-        nc.gpsimd.memset(planes[:].bitcast(I32), 0)
-        nc.gpsimd.memset(w2_plane[:].bitcast(I32), 0)
+        nc.vector.memset(planes[:].bitcast(I32), 0)
+        nc.vector.memset(w2_plane[:].bitcast(I32), 0)
         words = load_words(0, SLOT)
         nc.sync.dma_start(offsets[:], offs)
         for q in range(4):
@@ -119,8 +119,6 @@ def tile_list_tabres_none_kernel(tc, tab_words, tab_scales, w1, w2_words, w2_sca
                 out=planes[32 * q : 32 * q + 4 * PASSES, :].bitcast(I32), in_=tab_scales[:, 4 * q : 4 * q + 4, :].bitcast(I32)
             )
         raw = load_w1(0, 4 * SLOT)
-        for q in range(4):
-            nc.gpsimd.dma_start(out=w2_plane[32 * q : 32 * q + 4, :].bitcast(I32), in_=w2_scales[0, 4 * q : 4 * q + 4, :].bitcast(I32))
         picked[0] = shared("picked0", [P, S], U32)
         gather_words(0, words, 0, S)
         picked_planes = placed("picked_planes", [P, S], U8, SLOT + 2048)
@@ -129,6 +127,8 @@ def tile_list_tabres_none_kernel(tc, tab_words, tab_scales, w1, w2_words, w2_sca
         for c in range(S // CHUNK):
             first_product(0, c)
         words = load_words(1, 6 * SLOT)
+        for q in range(4):
+            nc.sync.dma_start(out=w2_plane[32 * q : 32 * q + 4, :].bitcast(I32), in_=w2_scales[0, 4 * q : 4 * q + 4, :].bitcast(I32))
         raw = load_w1(1, SLOT - 7168)
         picked[1] = shared("w1_bf0_0", [P, S], U32)
         gather_words(1, words, 0, HALF)

@@ -1,6 +1,7 @@
 from contextlib import ExitStack
 
 import concourse.mybir as mybir
+from concourse.masks import make_identity
 
 K, H, M, T, S = 1536, 512, 512, 2048, 1024
 FLOPS = 2 * K * H * S + 2 * H * M * S
@@ -146,9 +147,9 @@ def tile_list_tabres_none_kernel(tc, tab_words, tab_scales, w1, w2_words, w2_sca
 
         y, got = {}, {}
 
-        def second_product(u):
+        def second_product(u, blocks):
             nc.vector.quantize_mx(out=h_codes[u][:].bitcast(FP8X4), scales=h_plane[u][:], in_=h_bf[u][:])
-            for n in range(BLOCKS):
+            for n in blocks:
                 y[n, u] = psum.tile([P, HALF], F32, name="y%d_%d" % (n, u), tag="bank%d" % (4 * u + n))
                 nc.tensor.matmul_mx(
                     out=y[n, u][:],
@@ -167,31 +168,69 @@ def tile_list_tabres_none_kernel(tc, tab_words, tab_scales, w1, w2_words, w2_sca
         def store(n, first, count, res):
             nc.sync.dma_start(out=out[P * n : P * (n + 1), first : first + count], in_=res[:])
 
+        identity = shared("identity", [P, P], F32)
+        make_identity(nc, identity[:])
+        staged, turned, back = {}, {}, {}
+
+        def stage(n, u):
+            staged[n, u] = shared("staged%d_%d" % (n, u), [P, HALF], F32)
+            nc.scalar.copy(staged[n, u][:], y[n, u][:])
+
+        def finish_fused(n, u, counts=(HALF,), tag=None):
+            done = 0
+            for count in counts:
+                res = shared(tag or "res%d_%d_%d" % (n, u, done), [P, count], F32)
+                first = HALF * u + done
+                nc.vector.tensor_tensor(res[:], resid[n][:].indirect(listed(first, count)), staged[n, u][:, done : done + count], ADD)
+                store(n, first, count, res)
+                done = done + count
+
         def finish_on_vector(n, u):
             res = shared("res%d_%d" % (n, u), [P, HALF], F32)
             nc.vector.tensor_tensor(res[:], y[n, u][:], got[n, u][:], ADD)
             store(n, HALF * u, HALF, res)
 
-        def finish_fused(n, u, counts=(HALF,)):
-            staged = shared("staged%d_%d" % (n, u), [P, HALF], F32)
-            nc.scalar.copy(staged[:], y[n, u][:])
-            done = 0
-            for count in counts:
-                res = shared("res%d_%d_%d" % (n, u, done), [P, count], F32)
-                first = HALF * u + done
-                nc.vector.tensor_tensor(res[:], resid[n][:].indirect(listed(first, count)), staged[:, done : done + count], ADD)
-                store(n, first, count, res)
-                done = done + count
+        def turn_and_add(u, bank):
+            turned[u] = psum.tile([P, HALF], F32, name="turned%d" % u, tag="bank%d" % bank)
+            for k, part in enumerate((got[0, u], staged[0, u])):
+                for b in range(HALF // P):
+                    cols = slice(P * b, P * (b + 1))
+                    nc.tensor.matmul(
+                        turned[u][:, cols], part[:, cols], identity[:], is_transpose=True,
+                        start=(k == 0 and b == 0), stop=(k == 1 and b == HALF // P - 1),
+                    )
+
+        def turn_back(u, bank):
+            total = shared("total%d" % u, [P, HALF], F32)
+            nc.scalar.copy(total[:], turned[u][:])
+            back[u] = psum.tile([P, HALF], F32, name="back%d" % u, tag="bank%d" % bank)
+            for b in range(HALF // P):
+                cols = slice(P * b, P * (b + 1))
+                nc.tensor.transpose(back[u][:, cols], total[:, cols], identity[:])
+
+        def finish_turned(u):
+            res = shared("res0_%d" % u, [P, HALF], F32)
+            nc.scalar.copy(res[:], back[u][:])
+            store(0, HALF * u, HALF, res)
 
         gather_resid(0, 0, "got00")
-        second_product(0)
+        second_product(0, (0, 1, 2, 3))
         gather_resid(0, 1, "h_bf0")
         finish_on_vector(0, 0)
-        second_product(1)
+        second_product(1, (1, 0, 2, 3))
+        stage(1, 0)
         finish_fused(1, 0)
+        stage(2, 0)
         finish_fused(2, 0)
-        finish_on_vector(0, 1)
-        finish_fused(1, 1)
+        stage(1, 1)
+        finish_fused(1, 1, tag="staged2_0")
+        stage(3, 0)
+        stage(0, 1)
+        turn_and_add(1, 3)
+        stage(2, 1)
         finish_fused(2, 1)
+        turn_back(1, 1)
         finish_fused(3, 0)
+        stage(3, 1)
+        finish_turned(1)
         finish_fused(3, 1, (256, 256))

@@ -128,8 +128,6 @@ def tile_list_tabres_none_kernel(tc, tab_words, tab_scales, w1, w2_words, w2_sca
         for c in range(S // CHUNK):
             first_product(0, c)
         words = load_words(1, 6 * SLOT)
-        for q in range(4):
-            nc.sync.dma_start(out=w2_plane[32 * q : 32 * q + 4, :].bitcast(I32), in_=w2_scales[0, 4 * q : 4 * q + 4, :].bitcast(I32))
         raw = load_w1(1, SLOT - 7168)
         picked[1] = shared("w1_bf0_0", [P, S], U32)
         gather_words(1, words, 0, HALF)
@@ -143,6 +141,8 @@ def tile_list_tabres_none_kernel(tc, tab_words, tab_scales, w1, w2_words, w2_sca
         resid = [load_resid(0, 4 * SLOT)]
         w2_codes = shared("w1_bf0_1", [P, 2 * M], U8)
         nc.sync.dma_start(out=w2_codes[:].bitcast(I32), in_=w2_words[0].bitcast(I32))
+        for q in range(4):
+            nc.sync.dma_start(out=w2_plane[32 * q : 32 * q + 4, :].bitcast(I32), in_=w2_scales[0, 4 * q : 4 * q + 4, :].bitcast(I32))
         resid = resid + [load_resid(n + 1, at) for n, at in enumerate((6 * SLOT - 7168, 6 * SLOT + 7168, SLOT - 7168))]
 
         y, got = {}, {}

@@ -64,9 +64,9 @@ def tile_list_tabres_none_kernel(tc, tab_words, tab_scales, w1, w2_words, w2_sca
         picked = {}
         w1_codes = [shared("w1_codes%d" % a, [P, H], U32) for a in range(PASSES)]
         w1_plane = [shared("w1_plane%d" % a, [P, H], U8) for a in range(PASSES)]
-        h_bf = [shared("h_bf%d" % u, [P, HALF * PACK], BF16) for u in range(2)]
+        h_bf = [shared("h_bf0", [P, HALF * PACK], BF16), shared("h_bf1", [P, HALF * PACK // 2], BF16)]
         h_codes = [shared("h_codes%d" % u, [P, HALF], U32) for u in range(2)]
-        h_plane = [shared("h_plane%d" % u, [P, HALF], U8) for u in range(2)]
+        h_plane = [shared("h_plane0", [P, HALF], U8), shared("h_plane1", [P, HALF], U8)]
         banks = [psum.tile([P, PACK, CHUNK], F32, name="bank%d" % c, tag="bank%d" % c) for c in range(S // CHUNK)]
 
         def prepare_w1(a, raw, copies):
@@ -95,7 +95,8 @@ def tile_list_tabres_none_kernel(tc, tab_words, tab_scales, w1, w2_words, w2_sca
                 )
 
         def relu(c):
-            dst = h_bf[c // 4][:, (c % 4) * 512 : (c % 4 + 1) * 512].rearrange("p (n t) -> p n t", t=PACK)
+            piece, at = (0, c) if c < 4 else (c // 2 - 1, c % 2)
+            dst = h_bf[piece][:, at * 512 : (at + 1) * 512].rearrange("p (n t) -> p n t", t=PACK)
             nc.scalar.activation(dst, banks[c][:].rearrange("p t n -> p n t"), RELU)
 
         def gather_words(a, words, first, count):
@@ -107,7 +108,7 @@ def tile_list_tabres_none_kernel(tc, tab_words, tab_scales, w1, w2_words, w2_sca
                 gather_words(a, words, first, count)
                 for c in range(first // CHUNK, (first + count) // CHUNK):
                     first_product(a, c)
-                    if a == PASSES - 1:
+                    if a == PASSES - 1 and c < 6:
                         relu(c)
                 first = first + count
 
@@ -147,8 +148,10 @@ def tile_list_tabres_none_kernel(tc, tab_words, tab_scales, w1, w2_words, w2_sca
 
         y, got = {}, {}
 
+        def quantise_h(piece, u, cols):
+            nc.vector.quantize_mx(out=h_codes[u][:, cols].bitcast(FP8X4), scales=h_plane[u][:, cols], in_=h_bf[piece][:])
+
         def second_product(u, blocks):
-            nc.vector.quantize_mx(out=h_codes[u][:].bitcast(FP8X4), scales=h_plane[u][:], in_=h_bf[u][:])
             for n in blocks:
                 y[n, u] = psum.tile([P, HALF], F32, name="y%d_%d" % (n, u), tag="bank%d" % (4 * u + n))
                 nc.tensor.matmul_mx(
@@ -165,15 +168,15 @@ def tile_list_tabres_none_kernel(tc, tab_words, tab_scales, w1, w2_words, w2_sca
             got[n, u] = shared(tag, [P, HALF], F32)
             nc.vector.tensor_copy(got[n, u][:], resid[n][:].indirect(listed(HALF * u, HALF)))
 
-        def store(n, first, count, res):
-            nc.sync.dma_start(out=out[P * n : P * (n + 1), first : first + count], in_=res[:])
+        def store(queue, n, first, count, res):
+            queue.dma_start(out=out[P * n : P * (n + 1), first : first + count], in_=res[:])
 
         identity = shared("identity", [P, P], F32)
         make_identity(nc, identity[:])
         staged, turned, back = {}, {}, {}
 
-        def stage(n, u):
-            staged[n, u] = shared("staged%d_%d" % (n, u), [P, HALF], F32)
+        def stage(n, u, tag=None):
+            staged[n, u] = shared(tag or "staged%d_%d" % (n, u), [P, HALF], F32)
             nc.scalar.copy(staged[n, u][:], y[n, u][:])
 
         def finish_fused(n, u, counts=(HALF,), tag=None):
@@ -182,23 +185,18 @@ def tile_list_tabres_none_kernel(tc, tab_words, tab_scales, w1, w2_words, w2_sca
                 res = shared(tag or "res%d_%d_%d" % (n, u, done), [P, count], F32)
                 first = HALF * u + done
                 nc.vector.tensor_tensor(res[:], resid[n][:].indirect(listed(first, count)), staged[n, u][:, done : done + count], ADD)
-                store(n, first, count, res)
+                store(nc.sync, n, first, count, res)
                 done = done + count
 
-        def finish_on_vector(n, u):
-            res = shared("res%d_%d" % (n, u), [P, HALF], F32)
-            nc.vector.tensor_tensor(res[:], y[n, u][:], got[n, u][:], ADD)
-            store(n, HALF * u, HALF, res)
-
-        def turn_and_add(u, bank):
-            turned[u] = psum.tile([P, HALF], F32, name="turned%d" % u, tag="bank%d" % bank)
-            for k, part in enumerate((got[0, u], staged[0, u])):
-                for b in range(HALF // P):
-                    cols = slice(P * b, P * (b + 1))
-                    nc.tensor.matmul(
-                        turned[u][:, cols], part[:, cols], identity[:], is_transpose=True,
-                        start=(k == 0 and b == 0), stop=(k == 1 and b == HALF // P - 1),
-                    )
+        def turn(u, part, first, bank=None):
+            if first:
+                turned[u] = psum.tile([P, HALF], F32, name="turned%d" % u, tag="bank%d" % bank)
+            for b in range(HALF // P):
+                cols = slice(P * b, P * (b + 1))
+                nc.tensor.matmul(
+                    turned[u][:, cols], part[:, cols], identity[:], is_transpose=True,
+                    start=(first and b == 0), stop=(not first and b == HALF // P - 1),
+                )
 
         def turn_back(u, bank):
             total = shared("total%d" % u, [P, HALF], F32)
@@ -211,26 +209,37 @@ def tile_list_tabres_none_kernel(tc, tab_words, tab_scales, w1, w2_words, w2_sca
         def finish_turned(u):
             res = shared("res0_%d" % u, [P, HALF], F32)
             nc.scalar.copy(res[:], back[u][:])
-            store(0, HALF * u, HALF, res)
+            store(nc.scalar, 0, HALF * u, HALF, res)
 
         gather_resid(0, 0, "got00")
-        second_product(0, (0, 1, 2, 3))
+        quantise_h(0, 0, slice(0, HALF))
+        second_product(0, (1, 2, 0, 3))
         gather_resid(0, 1, "h_bf0")
-        finish_on_vector(0, 0)
-        second_product(1, (1, 0, 2, 3))
+        quantise_h(1, 1, slice(0, 256))
+        h_bf.append(shared("h_bf2", [P, HALF * PACK // 2], BF16))
+        relu(6)
+        relu(7)
+        quantise_h(2, 1, slice(256, HALF))
+        second_product(1, (1, 2, 0, 3))
         stage(1, 0)
         finish_fused(1, 0)
+        turn(0, got[0, 0], True, 1)
         stage(2, 0)
         finish_fused(2, 0)
+        stage(0, 0)
+        turn(0, staged[0, 0], False)
+        turn(1, got[0, 1], True, 0)
         stage(1, 1)
         finish_fused(1, 1, tag="staged2_0")
-        stage(3, 0)
-        stage(0, 1)
-        turn_and_add(1, 3)
         stage(2, 1)
         finish_fused(2, 1)
-        turn_back(1, 1)
+        turn_back(0, 2)
+        stage(3, 0)
         finish_fused(3, 0)
+        stage(0, 1)
+        turn(1, staged[0, 1], False)
+        finish_turned(0)
         stage(3, 1)
+        turn_back(1, 5)
         finish_turned(1)
         finish_fused(3, 1, (256, 256))

@@ -80,6 +80,14 @@ def tile_list_tabres_none_kernel(tc, tab_words, tab_scales, w1, w2_words, w2_sca
                 cols = slice(256 * v, 256 * (v + 1))
                 nc.vector.quantize_mx(out=w1_codes[a][:, cols].bitcast(FP8X4), scales=w1_plane[a][:, cols], in_=bf[:])
 
+        def prepare_w1_shared(a, raw, split):
+            bf = shared("w1_bf%d" % a, [P, PACK * H], BF16)
+            src = raw[:].rearrange("p j (m t) -> p m t j", t=PACK)
+            dst = bf[:].rearrange("p (t m j) -> p m t j", t=PACK, j=PACK)
+            nc.vector.tensor_copy(dst[:, :split], src[:, :split])
+            nc.scalar.copy(dst[:, split:], src[:, split:])
+            nc.vector.quantize_mx(out=w1_codes[a][:].bitcast(FP8X4), scales=w1_plane[a][:], in_=bf[:])
+
         def first_product(a, c):
             cols = slice(CHUNK * c, CHUNK * (c + 1))
             for t in range(PACK):
@@ -129,14 +137,14 @@ def tile_list_tabres_none_kernel(tc, tab_words, tab_scales, w1, w2_words, w2_sca
         for c in range(S // CHUNK):
             first_product(0, c)
         words = load_words(1, 6 * SLOT)
-        raw = load_w1(1, SLOT - 7168)
+        raw = load_w1(1, 8 * SLOT)
         picked[1] = shared("w1_bf0_0", [P, S], U32)
         gather_words(1, words, 0, HALF)
         gather_words(1, words, HALF, HALF)
-        prepare_w1(1, raw, (nc.vector.tensor_copy, nc.scalar.copy))
+        prepare_w1_shared(1, raw, 32)
         for c in range(S // CHUNK):
             first_product(1, c)
-        prepare_w1(2, load_w1(2, SLOT + 7168), (nc.vector.tensor_copy, nc.scalar.copy))
+        prepare_w1_shared(2, load_w1(2, SLOT + 7168), 64)
         picked[2] = shared("picked2", [P, S], U32)
         gather_and_multiply(2, load_words(2, 3 * SLOT + 1024), (256, 256, 512))
         resid = [load_resid(0, 4 * SLOT)]
@@ -144,7 +152,7 @@ def tile_list_tabres_none_kernel(tc, tab_words, tab_scales, w1, w2_words, w2_sca
         nc.sync.dma_start(out=w2_codes[:].bitcast(I32), in_=w2_words[0].bitcast(I32))
         for q in range(4):
             nc.sync.dma_start(out=w2_plane[32 * q : 32 * q + 4, :].bitcast(I32), in_=w2_scales[0, 4 * q : 4 * q + 4, :].bitcast(I32))
-        resid = resid + [load_resid(n + 1, at) for n, at in enumerate((6 * SLOT - 7168, 6 * SLOT + 7168, SLOT - 7168))]
+        resid = resid + [load_resid(n + 1, at) for n, at in enumerate((6 * SLOT - 7168, 6 * SLOT + 7168, 8 * SLOT))]
 
         y, got = {}, {}
 

@@ -228,7 +228,7 @@ def tile_list_tabres_none_kernel(tc, tab_words, tab_scales, w1, w2_words, w2_sca
         relu(6)
         relu(7)
         quantise_h(2, 1, slice(256, HALF))
-        second_product(1, (1, 2, 0, 3))
+        second_product(1, (2, 0, 1, 3))
         stage(1, 0)
         finish_fused(1, 0)
         turn(0, got[0, 0], True, 1)
@@ -237,17 +237,17 @@ def tile_list_tabres_none_kernel(tc, tab_words, tab_scales, w1, w2_words, w2_sca
         stage(0, 0)
         turn(0, staged[0, 0], False)
         turn(1, got[0, 1], True, 0)
-        stage(1, 1)
-        finish_fused(1, 1, tag="staged2_0")
         stage(2, 1)
         finish_fused(2, 1)
-        turn_back(0, 2)
-        stage(3, 0)
-        finish_fused(3, 0)
         stage(0, 1)
         turn(1, staged[0, 1], False)
+        stage(1, 1)
+        finish_fused(1, 1, tag="staged2_0")
+        turn_back(0, 2)
+        turn_back(1, 6)
+        stage(3, 0)
+        finish_fused(3, 0)
         finish_turned(0)
         stage(3, 1)
-        turn_back(1, 5)
         finish_turned(1)
         finish_fused(3, 1, (256, 256))

@@ -141,12 +141,12 @@ def tile_list_tabres_none_kernel(tc, tab_words, tab_scales, w1, w2_words, w2_sca
         picked[1] = shared("w1_bf0_0", [P, S], U32)
         gather_words(1, words, 0, HALF)
         gather_words(1, words, HALF, HALF)
-        prepare_w1_shared(1, raw, 32)
+        prepare_w1_shared(1, raw, 48)
         for c in range(S // CHUNK):
             first_product(1, c)
-        prepare_w1_shared(2, load_w1(2, SLOT + 7168), 64)
+        prepare_w1_shared(2, load_w1(2, 9 * SLOT), 64)
         picked[2] = shared("picked2", [P, S], U32)
-        gather_and_multiply(2, load_words(2, 3 * SLOT + 1024), (256, 256, 512))
+        gather_and_multiply(2, load_words(2, 10 * SLOT), (256, 256, 512))
         resid = [load_resid(0, 4 * SLOT)]
         w2_codes = shared("w1_bf0_1", [P, 2 * M], U8)
         nc.sync.dma_start(out=w2_codes[:].bitcast(I32), in_=w2_words[0].bitcast(I32))

@@ -73,8 +73,8 @@ def tile_list_tabres_none_kernel(tc, tab_words, tab_scales, w1, w2_words, w2_sca
             halves = []
             for v, copy in enumerate(copies):
                 bf = shared("w1_bf%d_%d" % (a, v), [P, PACK * H // 2], BF16)
-                src = raw[:].rearrange("p j (m t) -> p m t j", t=PACK)[:, :, 2 * v : 2 * v + 2, :]
-                copy(bf[:].rearrange("p (t m j) -> p m t j", t=2, j=PACK), src)
+                src = raw[:].rearrange("p j (m t) -> p m j t", t=PACK)[:, :, :, 2 * v : 2 * v + 2]
+                copy(bf[:].rearrange("p (t m j) -> p m j t", t=2, j=PACK), src)
                 halves.append(bf)
             for v, bf in enumerate(halves):
                 cols = slice(256 * v, 256 * (v + 1))
@@ -82,8 +82,8 @@ def tile_list_tabres_none_kernel(tc, tab_words, tab_scales, w1, w2_words, w2_sca
 
         def prepare_w1_shared(a, raw, split):
             bf = shared("w1_bf%d" % a, [P, PACK * H], BF16)
-            src = raw[:].rearrange("p j (m t) -> p m t j", t=PACK)
-            dst = bf[:].rearrange("p (t m j) -> p m t j", t=PACK, j=PACK)
+            src = raw[:].rearrange("p j (m t) -> p m j t", t=PACK)
+            dst = bf[:].rearrange("p (t m j) -> p m j t", t=PACK, j=PACK)
             nc.vector.tensor_copy(dst[:, :split], src[:, :split])
             nc.scalar.copy(dst[:, split:], src[:, split:])
             nc.vector.quantize_mx(out=w1_codes[a][:].bitcast(FP8X4), scales=w1_plane[a][:], in_=bf[:])

@@ -88,9 +88,9 @@ def tile_list_tabres_none_kernel(tc, tab_words, tab_scales, w1, w2_words, w2_sca
             nc.scalar.copy(dst[:, split:], src[:, split:])
             nc.vector.quantize_mx(out=w1_codes[a][:].bitcast(FP8X4), scales=w1_plane[a][:], in_=bf[:])
 
-        def first_product(a, c):
+        def first_product(a, c, slots=range(PACK)):
             cols = slice(CHUNK * c, CHUNK * (c + 1))
-            for t in range(PACK):
+            for t in slots:
                 wcols = slice(P * t, P * (t + 1))
                 nc.tensor.matmul_mx(
                     out=banks[c][:, t, :],
@@ -134,17 +134,17 @@ def tile_list_tabres_none_kernel(tc, tab_words, tab_scales, w1, w2_words, w2_sca
         picked_planes = placed("picked_planes", [P, S], U8, SLOT + 2048)
         nc.vector.tensor_copy(picked_planes[:], planes[:].indirect(offsets[:]))
         prepare_w1(0, raw, (nc.scalar.copy, nc.scalar.copy))
-        for c in range(S // CHUNK):
-            first_product(0, c)
+        for pair in ((0, 1), (2, 3)):
+            for c in range(S // CHUNK):
+                first_product(0, c, pair)
         words = load_words(1, 6 * SLOT)
         raw = load_w1(1, 8 * SLOT)
         picked[1] = shared("w1_bf0_0", [P, S], U32)
-        gather_words(1, words, 0, HALF)
-        gather_words(1, words, HALF, HALF)
+        gather_words(1, words, 0, S)
         prepare_w1_shared(1, raw, 48)
         for c in range(S // CHUNK):
             first_product(1, c)
-        prepare_w1_shared(2, load_w1(2, 9 * SLOT), 64)
+        prepare_w1_shared(2, load_w1(2, 9 * SLOT), 56)
         picked[2] = shared("picked2", [P, S], U32)
         gather_and_multiply(2, load_words(2, 10 * SLOT), (256, 256, 512))
         resid = [load_resid(0, 4 * SLOT)]

@@ -64,7 +64,7 @@ def tile_list_tabres_none_kernel(tc, tab_words, tab_scales, w1, w2_words, w2_sca
         picked = {}
         w1_codes = [shared("w1_codes%d" % a, [P, H], U32) for a in range(PASSES)]
         w1_plane = [shared("w1_plane%d" % a, [P, H], U8) for a in range(PASSES)]
-        h_bf = [shared("h_bf0", [P, HALF * PACK], BF16), shared("h_bf1", [P, HALF * PACK // 2], BF16)]
+        h_bf = [shared("h_bf%d" % u, [P, HALF * PACK], BF16) for u in range(2)]
         h_codes = [shared("h_codes%d" % u, [P, HALF], U32) for u in range(2)]
         h_plane = [shared("h_plane0", [P, HALF], U8), shared("h_plane1", [P, HALF], U8)]
         banks = [psum.tile([P, PACK, CHUNK], F32, name="bank%d" % c, tag="bank%d" % c) for c in range(S // CHUNK)]
@@ -103,9 +103,13 @@ def tile_list_tabres_none_kernel(tc, tab_words, tab_scales, w1, w2_words, w2_sca
                 )
 
         def relu(c):
-            piece, at = (0, c) if c < 4 else (c // 2 - 1, c % 2)
+            piece, at = divmod(c, 4)
             dst = h_bf[piece][:, at * 512 : (at + 1) * 512].rearrange("p (n t) -> p n t", t=PACK)
-            nc.scalar.activation(dst, banks[c][:].rearrange("p t n -> p n t"), RELU)
+            src = banks[c][:].rearrange("p t n -> p n t")
+            if c == 3:
+                nc.vector.tensor_scalar_max(dst, src, 0.0)
+            else:
+                nc.scalar.activation(dst, src, RELU)
 
         def gather_words(a, words, first, count):
             nc.vector.tensor_copy(picked[a][:, first : first + count], words[:].indirect(listed(first, count)))
@@ -116,9 +120,9 @@ def tile_list_tabres_none_kernel(tc, tab_words, tab_scales, w1, w2_words, w2_sca
                 gather_words(a, words, first, count)
                 for c in range(first // CHUNK, (first + count) // CHUNK):
                     first_product(a, c)
-                    if a == PASSES - 1 and c < 6:
-                        relu(c)
                 first = first + count
+            for c in range(S // CHUNK):
+                relu(c)
 
         nc.vector.memset(planes[:].bitcast(I32), 0)
         nc.vector.memset(w2_plane[:].bitcast(I32), 0)
@@ -223,11 +227,7 @@ def tile_list_tabres_none_kernel(tc, tab_words, tab_scales, w1, w2_words, w2_sca
         quantise_h(0, 0, slice(0, HALF))
         second_product(0, (1, 2, 0, 3))
         gather_resid(0, 1, "h_bf0")
-        quantise_h(1, 1, slice(0, 256))
-        h_bf.append(shared("h_bf2", [P, HALF * PACK // 2], BF16))
-        relu(6)
-        relu(7)
-        quantise_h(2, 1, slice(256, HALF))
+        quantise_h(1, 1, slice(0, HALF))
         second_product(1, (2, 0, 1, 3))
         stage(1, 0)
         finish_fused(1, 0)

@@ -107,7 +107,8 @@ def tile_list_tabres_none_kernel(tc, tab_words, tab_scales, w1, w2_words, w2_sca
             dst = h_bf[piece][:, at * 512 : (at + 1) * 512].rearrange("p (n t) -> p n t", t=PACK)
             src = banks[c][:].rearrange("p t n -> p n t")
             if c == 3:
-                nc.vector.tensor_scalar_max(dst, src, 0.0)
+                nc.vector.tensor_scalar_max(dst[:, 64:], src[:, 64:], 0.0)
+                nc.scalar.activation(dst[:, :64], src[:, :64], RELU)
             else:
                 nc.scalar.activation(dst, src, RELU)
 
@@ -226,7 +227,7 @@ def tile_list_tabres_none_kernel(tc, tab_words, tab_scales, w1, w2_words, w2_sca
         gather_resid(0, 0, "got00")
         quantise_h(0, 0, slice(0, HALF))
         second_product(0, (1, 2, 0, 3))
-        gather_resid(0, 1, "h_bf0")
+        gather_resid(0, 1, "picked2")
         quantise_h(1, 1, slice(0, HALF))
         second_product(1, (2, 0, 1, 3))
         stage(1, 0)

@@ -80,13 +80,18 @@ def tile_list_tabres_none_kernel(tc, tab_words, tab_scales, w1, w2_words, w2_sca
                 cols = slice(256 * v, 256 * (v + 1))
                 nc.vector.quantize_mx(out=w1_codes[a][:, cols].bitcast(FP8X4), scales=w1_plane[a][:, cols], in_=bf[:])
 
-        def prepare_w1_shared(a, raw, split):
+        def prepare_w1_shared(a, raw, split, pieces):
             bf = shared("w1_bf%d" % a, [P, PACK * H], BF16)
             src = raw[:].rearrange("p j (m t) -> p m j t", t=PACK)
             dst = bf[:].rearrange("p (t m j) -> p m j t", t=PACK, j=PACK)
             nc.vector.tensor_copy(dst[:, :split], src[:, :split])
             nc.scalar.copy(dst[:, split:], src[:, split:])
-            nc.vector.quantize_mx(out=w1_codes[a][:].bitcast(FP8X4), scales=w1_plane[a][:], in_=bf[:])
+            width = H // pieces
+            for v in range(pieces):
+                cols = slice(width * v, width * (v + 1))
+                nc.vector.quantize_mx(
+                    out=w1_codes[a][:, cols].bitcast(FP8X4), scales=w1_plane[a][:, cols], in_=bf[:, PACK * width * v : PACK * width * (v + 1)]
+                )
 
         def first_product(a, c, slots=range(PACK)):
             cols = slice(CHUNK * c, CHUNK * (c + 1))
@@ -107,8 +112,8 @@ def tile_list_tabres_none_kernel(tc, tab_words, tab_scales, w1, w2_words, w2_sca
             dst = h_bf[piece][:, at * 512 : (at + 1) * 512].rearrange("p (n t) -> p n t", t=PACK)
             src = banks[c][:].rearrange("p t n -> p n t")
             if c == 3:
-                nc.vector.tensor_scalar_max(dst[:, 64:], src[:, 64:], 0.0)
-                nc.scalar.activation(dst[:, :64], src[:, :64], RELU)
+                nc.vector.tensor_scalar_max(dst[:, 56:], src[:, 56:], 0.0)
+                nc.scalar.activation(dst[:, :56], src[:, :56], RELU)
             else:
                 nc.scalar.activation(dst, src, RELU)
 
@@ -146,10 +151,11 @@ def tile_list_tabres_none_kernel(tc, tab_words, tab_scales, w1, w2_words, w2_sca
         raw = load_w1(1, 8 * SLOT)
         picked[1] = shared("w1_bf0_0", [P, S], U32)
         gather_words(1, words, 0, S)
-        prepare_w1_shared(1, raw, 48)
-        for c in range(S // CHUNK):
-            first_product(1, c)
-        prepare_w1_shared(2, load_w1(2, 9 * SLOT), 56)
+        prepare_w1_shared(1, raw, 48, 2)
+        for pair in ((0, 1), (2, 3)):
+            for c in range(S // CHUNK):
+                first_product(1, c, pair)
+        prepare_w1_shared(2, load_w1(2, 9 * SLOT), 56, 1)
         picked[2] = shared("picked2", [P, S], U32)
         gather_and_multiply(2, load_words(2, 10 * SLOT), (256, 256, 512))
         resid = [load_resid(0, 4 * SLOT)]

@@ -19,11 +19,26 @@ ADD = mybir.AluOpType.add
 
 P = 128
 PACK = 4
-PASSES = K // (P * PACK)
+PASS = P * PACK
+PASSES = K // PASS
+QUADRANTS = 4
+GROUP = 16
 CHUNK = 128
-HALF = 512
-BLOCKS = M // P
-SLOT = 10240
+CHUNKS = S // CHUNK
+HALF = S // 2
+QUARTER = S // 4
+PAIRS = ((0, 1), (2, 3))
+
+VECTOR_CASTS = {1: 48, 2: 56}
+SHARED_CHUNK, SCALAR_TOKENS = 3, 56
+
+ROW = 4 * T
+SLOT = ROW + T
+WORDS_AT = (SLOT, 6 * SLOT, 10 * SLOT)
+W1_AT = (4 * SLOT, 8 * SLOT, 9 * SLOT)
+PLANES_AT = 3 * SLOT
+PICKED_PLANES_AT = WORDS_AT[0] + T
+RESID_AT = (W1_AT[0], WORDS_AT[1] - ROW + 1024, WORDS_AT[1] + ROW - 1024, W1_AT[1])
 
 
 def tile_list_tabres_none_kernel(tc, tab_words, tab_scales, w1, w2_words, w2_scales, rT, offs, out):
@@ -31,74 +46,77 @@ def tile_list_tabres_none_kernel(tc, tab_words, tab_scales, w1, w2_words, w2_sca
     with ExitStack() as ctx:
         keep = ctx.enter_context(tc.tile_pool(name="keep", bufs=1))
         psum = ctx.enter_context(tc.psum_pool(name="psum", bufs=1))
-
         arena = ctx.enter_context(tc.tile_pool(name="arena", bufs=1))
 
-        offsets = keep.tile([P, S // 16], U16, name="offsets")
+        offsets = keep.tile([P, S // GROUP], U16, name="offsets")
 
         def placed(name, shape, dtype, at):
             return arena.tile(shape, dtype, name=name, tag=name, align_bytes=64, offset=at)
 
-        def shared(tag, shape, dtype):
+        def tagged(tag, shape, dtype):
             return keep.tile(shape, dtype, name=tag, tag=tag, align_bytes=64)
 
+        def bank(name, shape, index):
+            return psum.tile(shape, F32, name=name, tag="bank%d" % index)
+
         def listed(first, count):
-            return offsets[:, first // 16 : (first + count) // 16]
+            return offsets[:, first // GROUP : (first + count) // GROUP]
 
-        def load_big(name, at, shape, dtype, src):
-            tile = placed(name, shape, dtype, at)
-            nc.sync.dma_start(out=tile[:].bitcast(I32) if dtype == U32 else tile[:], in_=src)
-            return tile
+        def load_w1(a):
+            raw = placed("w1_raw%d" % a, [P, PACK, H], F32, W1_AT[a])
+            nc.sync.dma_start(out=raw[:], in_=w1[PASS * a : PASS * (a + 1), :].rearrange("(p j) c -> p j c", j=PACK))
+            return raw
 
-        def load_w1(a, at):
-            return load_big("w1_raw%d" % a, at, [P, PACK, H], F32, w1[512 * a : 512 * (a + 1), :].rearrange("(p j) c -> p j c", j=PACK))
+        def load_words(a):
+            words = placed("words%d" % a, [P, T], U32, WORDS_AT[a])
+            nc.sync.dma_start(out=words[:].bitcast(I32), in_=tab_words[a].rearrange("p t i -> p (t i)").bitcast(I32))
+            return words
 
-        def load_words(a, at):
-            return load_big("words%d" % a, at, [P, T], U32, tab_words[a].rearrange("p t i -> p (t i)").bitcast(I32))
+        def load_resid(n):
+            block = placed("resid%d" % n, [P, T], F32, RESID_AT[n])
+            nc.sync.dma_start(out=block[:], in_=rT[P * n : P * (n + 1), :])
+            return block
 
-        def load_resid(n, at):
-            return load_big("resid%d" % n, at, [P, T], F32, rT[P * n : P * (n + 1), :])
-
-        planes = placed("planes", [P, T], U8, 3 * SLOT)
-        w2_plane = shared("w2_plane", [P, M], U8)
+        planes = placed("planes", [P, T], U8, PLANES_AT)
+        w2_plane = tagged("w2_plane", [P, M], U8)
         picked = {}
-        w1_codes = [shared("w1_codes%d" % a, [P, H], U32) for a in range(PASSES)]
-        w1_plane = [shared("w1_plane%d" % a, [P, H], U8) for a in range(PASSES)]
-        h_bf = [shared("h_bf%d" % u, [P, HALF * PACK], BF16) for u in range(2)]
-        h_codes = [shared("h_codes%d" % u, [P, HALF], U32) for u in range(2)]
-        h_plane = [shared("h_plane0", [P, HALF], U8), shared("h_plane1", [P, HALF], U8)]
-        banks = [psum.tile([P, PACK, CHUNK], F32, name="bank%d" % c, tag="bank%d" % c) for c in range(S // CHUNK)]
+        w1_codes = [tagged("w1_codes%d" % a, [P, H], U32) for a in range(PASSES)]
+        w1_plane = [tagged("w1_plane%d" % a, [P, H], U8) for a in range(PASSES)]
+        h_bf = [tagged("h_bf%d" % u, [P, HALF * PACK], BF16) for u in range(2)]
+        h_codes = [tagged("h_codes%d" % u, [P, HALF], U32) for u in range(2)]
+        h_plane = [tagged("h_plane%d" % u, [P, HALF], U8) for u in range(2)]
+        h_sum = [bank("bank%d" % c, [P, PACK, CHUNK], c) for c in range(CHUNKS)]
 
-        def prepare_w1(a, raw, copies):
-            halves = []
-            for v, copy in enumerate(copies):
-                bf = shared("w1_bf%d_%d" % (a, v), [P, PACK * H // 2], BF16)
-                src = raw[:].rearrange("p j (m t) -> p m j t", t=PACK)[:, :, :, 2 * v : 2 * v + 2]
-                copy(bf[:].rearrange("p (t m j) -> p m j t", t=2, j=PACK), src)
-                halves.append(bf)
-            for v, bf in enumerate(halves):
-                cols = slice(256 * v, 256 * (v + 1))
-                nc.vector.quantize_mx(out=w1_codes[a][:, cols].bitcast(FP8X4), scales=w1_plane[a][:, cols], in_=bf[:])
+        def quantise_w1(a, first, count, rounded):
+            cols = slice(first, first + count)
+            nc.vector.quantize_mx(out=w1_codes[a][:, cols].bitcast(FP8X4), scales=w1_plane[a][:, cols], in_=rounded)
 
-        def prepare_w1_shared(a, raw, split, pieces):
-            bf = shared("w1_bf%d" % a, [P, PACK * H], BF16)
+        def prepare_w1_on_scalar(a, raw):
             src = raw[:].rearrange("p j (m t) -> p m j t", t=PACK)
-            dst = bf[:].rearrange("p (t m j) -> p m j t", t=PACK, j=PACK)
+            rounded = []
+            for v, pair in enumerate(PAIRS):
+                rounded.append(tagged("w1_bf%d_%d" % (a, v), [P, PACK * H // 2], BF16))
+                nc.scalar.copy(rounded[v][:].rearrange("p (t m j) -> p m j t", t=2, j=PACK), src[:, :, :, pair[0] : pair[1] + 1])
+            for v in range(len(PAIRS)):
+                quantise_w1(a, v * H // 2, H // 2, rounded[v][:])
+
+        def prepare_w1_shared(a, raw, pieces):
+            rounded = tagged("w1_bf%d" % a, [P, PACK * H], BF16)
+            src = raw[:].rearrange("p j (m t) -> p m j t", t=PACK)
+            dst = rounded[:].rearrange("p (t m j) -> p m j t", t=PACK, j=PACK)
+            split = VECTOR_CASTS[a]
             nc.vector.tensor_copy(dst[:, :split], src[:, :split])
             nc.scalar.copy(dst[:, split:], src[:, split:])
             width = H // pieces
-            for v in range(pieces):
-                cols = slice(width * v, width * (v + 1))
-                nc.vector.quantize_mx(
-                    out=w1_codes[a][:, cols].bitcast(FP8X4), scales=w1_plane[a][:, cols], in_=bf[:, PACK * width * v : PACK * width * (v + 1)]
-                )
+            for first in range(0, H, width):
+                quantise_w1(a, first, width, rounded[:, PACK * first : PACK * (first + width)])
 
-        def first_product(a, c, slots=range(PACK)):
+        def first_product(a, c, row_sets):
             cols = slice(CHUNK * c, CHUNK * (c + 1))
-            for t in slots:
+            for t in row_sets:
                 wcols = slice(P * t, P * (t + 1))
                 nc.tensor.matmul_mx(
-                    out=banks[c][:, t, :],
+                    out=h_sum[c][:, t, :],
                     lhsT=w1_codes[a][:, wcols].bitcast(FP8X4),
                     lhsT_scale=w1_plane[a][:, wcols],
                     rhs=picked[a][:, cols].bitcast(FP8X4),
@@ -107,72 +125,72 @@ def tile_list_tabres_none_kernel(tc, tab_words, tab_scales, w1, w2_words, w2_sca
                     stop=(a == PASSES - 1 and t == PACK - 1),
                 )
 
+        def first_product_by_pairs(a):
+            for pair in PAIRS:
+                for c in range(CHUNKS):
+                    first_product(a, c, pair)
+
         def relu(c):
-            piece, at = divmod(c, 4)
-            dst = h_bf[piece][:, at * 512 : (at + 1) * 512].rearrange("p (n t) -> p n t", t=PACK)
-            src = banks[c][:].rearrange("p t n -> p n t")
-            if c == 3:
-                nc.vector.tensor_scalar_max(dst[:, 56:], src[:, 56:], 0.0)
-                nc.scalar.activation(dst[:, :56], src[:, :56], RELU)
+            u, at = divmod(c, CHUNKS // 2)
+            dst = h_bf[u][:, at * PACK * CHUNK : (at + 1) * PACK * CHUNK].rearrange("p (n t) -> p n t", t=PACK)
+            src = h_sum[c][:].rearrange("p t n -> p n t")
+            if c == SHARED_CHUNK:
+                nc.vector.tensor_scalar_max(dst[:, SCALAR_TOKENS:], src[:, SCALAR_TOKENS:], 0.0)
+                nc.scalar.activation(dst[:, :SCALAR_TOKENS], src[:, :SCALAR_TOKENS], RELU)
             else:
                 nc.scalar.activation(dst, src, RELU)
 
         def gather_words(a, words, first, count):
             nc.vector.tensor_copy(picked[a][:, first : first + count], words[:].indirect(listed(first, count)))
 
-        def gather_and_multiply(a, words, counts):
-            first = 0
-            for count in counts:
-                gather_words(a, words, first, count)
-                for c in range(first // CHUNK, (first + count) // CHUNK):
-                    first_product(a, c)
-                first = first + count
-            for c in range(S // CHUNK):
-                relu(c)
-
         nc.vector.memset(planes[:].bitcast(I32), 0)
         nc.vector.memset(w2_plane[:].bitcast(I32), 0)
-        words = load_words(0, SLOT)
+        words = load_words(0)
         nc.sync.dma_start(offsets[:], offs)
-        for q in range(4):
+        for q in range(QUADRANTS):
             (nc.sync if q % 2 else nc.scalar).dma_start(
                 out=planes[32 * q : 32 * q + 4 * PASSES, :].bitcast(I32), in_=tab_scales[:, 4 * q : 4 * q + 4, :].bitcast(I32)
             )
-        raw = load_w1(0, 4 * SLOT)
-        picked[0] = shared("picked0", [P, S], U32)
+        raw = load_w1(0)
+        picked[0] = tagged("picked0", [P, S], U32)
         gather_words(0, words, 0, S)
-        picked_planes = placed("picked_planes", [P, S], U8, SLOT + 2048)
+        picked_planes = placed("picked_planes", [P, S], U8, PICKED_PLANES_AT)
         nc.vector.tensor_copy(picked_planes[:], planes[:].indirect(offsets[:]))
-        prepare_w1(0, raw, (nc.scalar.copy, nc.scalar.copy))
-        for pair in ((0, 1), (2, 3)):
-            for c in range(S // CHUNK):
-                first_product(0, c, pair)
-        words = load_words(1, 6 * SLOT)
-        raw = load_w1(1, 8 * SLOT)
-        picked[1] = shared("w1_bf0_0", [P, S], U32)
+        prepare_w1_on_scalar(0, raw)
+        first_product_by_pairs(0)
+
+        words = load_words(1)
+        raw = load_w1(1)
+        picked[1] = tagged("w1_bf0_0", [P, S], U32)
         gather_words(1, words, 0, S)
-        prepare_w1_shared(1, raw, 48, 2)
-        for pair in ((0, 1), (2, 3)):
-            for c in range(S // CHUNK):
-                first_product(1, c, pair)
-        prepare_w1_shared(2, load_w1(2, 9 * SLOT), 56, 1)
-        picked[2] = shared("picked2", [P, S], U32)
-        gather_and_multiply(2, load_words(2, 10 * SLOT), (256, 256, 512))
-        resid = [load_resid(0, 4 * SLOT)]
-        w2_codes = shared("w1_bf0_1", [P, 2 * M], U8)
+        prepare_w1_shared(1, raw, len(PAIRS))
+        first_product_by_pairs(1)
+
+        prepare_w1_shared(2, load_w1(2), 1)
+        picked[2] = tagged("picked2", [P, S], U32)
+        words = load_words(2)
+        for first, count in ((0, QUARTER), (QUARTER, QUARTER), (HALF, HALF)):
+            gather_words(2, words, first, count)
+            for c in range(first // CHUNK, (first + count) // CHUNK):
+                first_product(2, c, range(PACK))
+        for c in range(CHUNKS):
+            relu(c)
+
+        resid = [load_resid(0)]
+        w2_codes = tagged("w1_bf0_1", [P, 2 * M], U8)
         nc.sync.dma_start(out=w2_codes[:].bitcast(I32), in_=w2_words[0].bitcast(I32))
-        for q in range(4):
+        for q in range(QUADRANTS):
             nc.sync.dma_start(out=w2_plane[32 * q : 32 * q + 4, :].bitcast(I32), in_=w2_scales[0, 4 * q : 4 * q + 4, :].bitcast(I32))
-        resid = resid + [load_resid(n + 1, at) for n, at in enumerate((6 * SLOT - 7168, 6 * SLOT + 7168, 8 * SLOT))]
+        resid = resid + [load_resid(n) for n in range(1, M // P)]
 
-        y, got = {}, {}
+        y, staged, early, turned, back = {}, {}, {}, {}, {}
 
-        def quantise_h(piece, u, cols):
-            nc.vector.quantize_mx(out=h_codes[u][:, cols].bitcast(FP8X4), scales=h_plane[u][:, cols], in_=h_bf[piece][:])
+        def quantise_h(u):
+            nc.vector.quantize_mx(out=h_codes[u][:].bitcast(FP8X4), scales=h_plane[u][:], in_=h_bf[u][:])
 
         def second_product(u, blocks):
             for n in blocks:
-                y[n, u] = psum.tile([P, HALF], F32, name="y%d_%d" % (n, u), tag="bank%d" % (4 * u + n))
+                y[n, u] = bank("y%d_%d" % (n, u), [P, HALF], 4 * u + n)
                 nc.tensor.matmul_mx(
                     out=y[n, u][:],
                     lhsT=w2_codes[:, 2 * P * n : 2 * P * (n + 1)].bitcast(FP4X4),
@@ -183,78 +201,78 @@ def tile_list_tabres_none_kernel(tc, tab_words, tab_scales, w1, w2_words, w2_sca
                     stop=True,
                 )
 
-        def gather_resid(n, u, tag):
-            got[n, u] = shared(tag, [P, HALF], F32)
-            nc.vector.tensor_copy(got[n, u][:], resid[n][:].indirect(listed(HALF * u, HALF)))
+        def gather_early(u, tag):
+            early[u] = tagged(tag, [P, HALF], F32)
+            nc.vector.tensor_copy(early[u][:], resid[0][:].indirect(listed(HALF * u, HALF)))
 
         def store(queue, n, first, count, res):
             queue.dma_start(out=out[P * n : P * (n + 1), first : first + count], in_=res[:])
 
-        identity = shared("identity", [P, P], F32)
+        identity = tagged("identity", [P, P], F32)
         make_identity(nc, identity[:])
-        staged, turned, back = {}, {}, {}
 
-        def stage(n, u, tag=None):
-            staged[n, u] = shared(tag or "staged%d_%d" % (n, u), [P, HALF], F32)
-            nc.scalar.copy(staged[n, u][:], y[n, u][:])
+        def stage(n, u, count=HALF):
+            staged[n, u] = tagged("staged%d_%d" % (n, u), [P, HALF], F32)
+            for first in range(0, HALF, count):
+                nc.scalar.copy(staged[n, u][:, first : first + count], y[n, u][:, first : first + count])
 
-        def finish_fused(n, u, counts=(HALF,), tag=None):
-            done = 0
-            for count in counts:
-                res = shared(tag or "res%d_%d_%d" % (n, u, done), [P, count], F32)
+        def gather_and_add(n, u, count=HALF, tag=None):
+            for done in range(0, HALF, count):
+                res = tagged(tag or "res%d_%d_%d" % (n, u, done), [P, count], F32)
                 first = HALF * u + done
                 nc.vector.tensor_tensor(res[:], resid[n][:].indirect(listed(first, count)), staged[n, u][:, done : done + count], ADD)
                 store(nc.sync, n, first, count, res)
-                done = done + count
 
-        def turn(u, part, first, bank=None):
-            if first:
-                turned[u] = psum.tile([P, HALF], F32, name="turned%d" % u, tag="bank%d" % bank)
+        def add_turned(u, term, opens):
             for b in range(HALF // P):
                 cols = slice(P * b, P * (b + 1))
                 nc.tensor.matmul(
-                    turned[u][:, cols], part[:, cols], identity[:], is_transpose=True,
-                    start=(first and b == 0), stop=(not first and b == HALF // P - 1),
+                    turned[u][:, cols], term[:, cols], identity[:], is_transpose=True,
+                    start=(opens and b == 0), stop=(not opens and b == HALF // P - 1),
                 )
 
-        def turn_back(u, bank):
-            total = shared("total%d" % u, [P, HALF], F32)
+        def turn_early(u, index):
+            turned[u] = bank("turned%d" % u, [P, HALF], index)
+            add_turned(u, early[u], True)
+
+        def turn_back(u, index):
+            total = tagged("total%d" % u, [P, HALF], F32)
             nc.scalar.copy(total[:], turned[u][:])
-            back[u] = psum.tile([P, HALF], F32, name="back%d" % u, tag="bank%d" % bank)
+            back[u] = bank("back%d" % u, [P, HALF], index)
             for b in range(HALF // P):
                 cols = slice(P * b, P * (b + 1))
                 nc.tensor.transpose(back[u][:, cols], total[:, cols], identity[:])
 
-        def finish_turned(u):
-            res = shared("res0_%d" % u, [P, HALF], F32)
+        def store_turned(u):
+            res = tagged("res0_%d" % u, [P, HALF], F32)
             nc.scalar.copy(res[:], back[u][:])
             store(nc.scalar, 0, HALF * u, HALF, res)
 
-        gather_resid(0, 0, "got00")
-        quantise_h(0, 0, slice(0, HALF))
+        gather_early(0, "early0")
+        quantise_h(0)
         second_product(0, (1, 2, 0, 3))
-        gather_resid(0, 1, "picked2")
-        quantise_h(1, 1, slice(0, HALF))
+        gather_early(1, "picked2")
+        quantise_h(1)
         second_product(1, (2, 0, 1, 3))
         stage(1, 0)
-        finish_fused(1, 0)
-        turn(0, got[0, 0], True, 1)
+        gather_and_add(1, 0)
+        turn_early(0, 1)
         stage(2, 0)
-        finish_fused(2, 0)
+        gather_and_add(2, 0)
         stage(0, 0)
-        turn(0, staged[0, 0], False)
-        turn(1, got[0, 1], True, 0)
+        add_turned(0, staged[0, 0], False)
+        turn_early(1, 0)
         stage(2, 1)
-        finish_fused(2, 1)
+        gather_and_add(2, 1)
         stage(0, 1)
-        turn(1, staged[0, 1], False)
-        stage(1, 1)
-        finish_fused(1, 1, tag="staged2_0")
+        add_turned(1, staged[0, 1], False)
         turn_back(0, 2)
+        stage(1, 1)
+        gather_and_add(1, 1, tag="staged2_0")
         turn_back(1, 6)
+        store_turned(0)
         stage(3, 0)
-        finish_fused(3, 0)
-        finish_turned(0)
-        stage(3, 1)
-        finish_turned(1)
-        finish_fused(3, 1, (256, 256))
+        gather_and_add(3, 0)
+        store_turned(1)
+        stage(3, 1, QUARTER)
+        gather_and_add(3, 1, QUARTER)

@@ -30,7 +30,8 @@ QUARTER = S // 4
 PAIRS = ((0, 1), (2, 3))
 
 VECTOR_CASTS = {1: 48, 2: 56}
-SHARED_CHUNK, SCALAR_TOKENS = 3, 56
+
+EARLY_FIRST = 512
 
 ROW = 4 * T
 SLOT = ROW + T
@@ -133,12 +134,7 @@ def tile_list_tabres_none_kernel(tc, tab_words, tab_scales, w1, w2_words, w2_sca
         def relu(c):
             u, at = divmod(c, CHUNKS // 2)
             dst = h_bf[u][:, at * PACK * CHUNK : (at + 1) * PACK * CHUNK].rearrange("p (n t) -> p n t", t=PACK)
-            src = h_sum[c][:].rearrange("p t n -> p n t")
-            if c == SHARED_CHUNK:
-                nc.vector.tensor_scalar_max(dst[:, SCALAR_TOKENS:], src[:, SCALAR_TOKENS:], 0.0)
-                nc.scalar.activation(dst[:, :SCALAR_TOKENS], src[:, :SCALAR_TOKENS], RELU)
-            else:
-                nc.scalar.activation(dst, src, RELU)
+            nc.scalar.activation(dst, h_sum[c][:].rearrange("p t n -> p n t"), RELU)
 
         def gather_words(a, words, first, count):
             nc.vector.tensor_copy(picked[a][:, first : first + count], words[:].indirect(listed(first, count)))
@@ -169,7 +165,7 @@ def tile_list_tabres_none_kernel(tc, tab_words, tab_scales, w1, w2_words, w2_sca
         prepare_w1_shared(2, load_w1(2), 1)
         picked[2] = tagged("picked2", [P, S], U32)
         words = load_words(2)
-        for first, count in ((0, QUARTER), (QUARTER, QUARTER), (HALF, HALF)):
+        for first, count in ((0, CHUNK), (CHUNK, CHUNK), (QUARTER, QUARTER), (HALF, HALF)):
             gather_words(2, words, first, count)
             for c in range(first // CHUNK, (first + count) // CHUNK):
                 first_product(2, c, range(PACK))
@@ -188,22 +184,23 @@ def tile_list_tabres_none_kernel(tc, tab_words, tab_scales, w1, w2_words, w2_sca
         def quantise_h(u):
             nc.vector.quantize_mx(out=h_codes[u][:].bitcast(FP8X4), scales=h_plane[u][:], in_=h_bf[u][:])
 
-        def second_product(u, blocks):
-            for n in blocks:
-                y[n, u] = bank("y%d_%d" % (n, u), [P, HALF], 4 * u + n)
-                nc.tensor.matmul_mx(
-                    out=y[n, u][:],
-                    lhsT=w2_codes[:, 2 * P * n : 2 * P * (n + 1)].bitcast(FP4X4),
-                    lhsT_scale=w2_plane[:, P * n : P * (n + 1)],
-                    rhs=h_codes[u][:].bitcast(FP8X4),
-                    rhs_scale=h_plane[u][:],
-                    start=True,
-                    stop=True,
-                )
+        def second_product(n, u, index):
+            y[n, u] = bank("y%d_%d" % (n, u), [P, HALF], index)
+            nc.tensor.matmul_mx(
+                out=y[n, u][:],
+                lhsT=w2_codes[:, 2 * P * n : 2 * P * (n + 1)].bitcast(FP4X4),
+                lhsT_scale=w2_plane[:, P * n : P * (n + 1)],
+                rhs=h_codes[u][:].bitcast(FP8X4),
+                rhs_scale=h_plane[u][:],
+                start=True,
+                stop=True,
+            )
 
-        def gather_early(u, tag):
-            early[u] = tagged(tag, [P, HALF], F32)
-            nc.vector.tensor_copy(early[u][:], resid[0][:].indirect(listed(HALF * u, HALF)))
+        def gather_early(first, count, tag):
+            picked_rows = tagged(tag, [P, count], F32)
+            nc.vector.tensor_copy(picked_rows[:], resid[0][:].indirect(listed(first, count)))
+            for at in range(0, count, P):
+                early[(first + at) // P] = picked_rows[:, at : at + P]
 
         def store(queue, n, first, count, res):
             queue.dma_start(out=out[P * n : P * (n + 1), first : first + count], in_=res[:])
@@ -223,17 +220,15 @@ def tile_list_tabres_none_kernel(tc, tab_words, tab_scales, w1, w2_words, w2_sca
                 nc.vector.tensor_tensor(res[:], resid[n][:].indirect(listed(first, count)), staged[n, u][:, done : done + count], ADD)
                 store(nc.sync, n, first, count, res)
 
-        def add_turned(u, term, opens):
-            for b in range(HALF // P):
-                cols = slice(P * b, P * (b + 1))
-                nc.tensor.matmul(
-                    turned[u][:, cols], term[:, cols], identity[:], is_transpose=True,
-                    start=(opens and b == 0), stop=(not opens and b == HALF // P - 1),
-                )
+        def squares(tile):
+            return [tile[:, P * b : P * (b + 1)] for b in range(HALF // P)]
 
-        def turn_early(u, index):
-            turned[u] = bank("turned%d" % u, [P, HALF], index)
-            add_turned(u, early[u], True)
+        def add_turned(u, first, term, start=False, stop=False):
+            for b, square in enumerate(term):
+                nc.tensor.matmul(
+                    turned[u][:, P * (first + b) : P * (first + b + 1)], square, identity[:], is_transpose=True,
+                    start=(start and b == 0), stop=(stop and b == len(term) - 1),
+                )
 
         def turn_back(u, index):
             total = tagged("total%d" % u, [P, HALF], F32)
@@ -243,36 +238,45 @@ def tile_list_tabres_none_kernel(tc, tab_words, tab_scales, w1, w2_words, w2_sca
                 cols = slice(P * b, P * (b + 1))
                 nc.tensor.transpose(back[u][:, cols], total[:, cols], identity[:])
 
-        def store_turned(u):
+        def fetch_turned(u):
             res = tagged("res0_%d" % u, [P, HALF], F32)
             nc.scalar.copy(res[:], back[u][:])
-            store(nc.scalar, 0, HALF * u, HALF, res)
+            return res
 
-        gather_early(0, "early0")
+        ahead = EARLY_FIRST // P
+        gather_early(0, EARLY_FIRST, "early")
         quantise_h(0)
-        second_product(0, (1, 2, 0, 3))
-        gather_early(1, "picked2")
+        turned[0] = bank("turned0", [P, HALF], 3)
+        add_turned(0, 0, [early[b] for b in range(ahead)], start=True)
+        for n in (1, 0, 2):
+            second_product(n, 0, n)
+        gather_early(EARLY_FIRST, S - EARLY_FIRST, "early")
         quantise_h(1)
-        second_product(1, (2, 0, 1, 3))
         stage(1, 0)
         gather_and_add(1, 0)
-        turn_early(0, 1)
+        turned[1] = bank("turned1", [P, HALF], 1)
+        add_turned(1, 0, [early[b] for b in range(HALF // P, S // P)], start=True)
+        stage(0, 0)
+        second_product(0, 1, 4)
+        second_product(2, 1, 6)
+        add_turned(0, 0, squares(staged[0, 0]), stop=True)
         stage(2, 0)
         gather_and_add(2, 0)
-        stage(0, 0)
-        add_turned(0, staged[0, 0], False)
-        turn_early(1, 0)
+        stage(0, 1)
+        add_turned(1, 0, squares(staged[0, 1]), stop=True)
+        second_product(1, 1, 5)
+        second_product(3, 0, 0)
         stage(2, 1)
         gather_and_add(2, 1)
-        stage(0, 1)
-        add_turned(1, staged[0, 1], False)
         turn_back(0, 2)
         stage(1, 1)
         gather_and_add(1, 1, tag="staged2_0")
-        turn_back(1, 6)
-        store_turned(0)
+        turn_back(1, 4)
+        second_product(3, 1, 7)
         stage(3, 0)
         gather_and_add(3, 0)
-        store_turned(1)
+        results = [fetch_turned(u) for u in range(2)]
+        store(nc.scalar, 0, 0, HALF, results[0])
         stage(3, 1, QUARTER)
+        store(nc.scalar, 0, HALF, HALF, results[1])
         gather_and_add(3, 1, QUARTER)

@@ -36,10 +36,11 @@ EARLY_FIRST = 512
 ROW = 4 * T
 SLOT = ROW + T
 WORDS_AT = (SLOT, 6 * SLOT, 10 * SLOT)
-W1_AT = (4 * SLOT, 8 * SLOT, 9 * SLOT)
+W1_AT = (4 * SLOT, 8 * SLOT, 11 * SLOT)
 PLANES_AT = 3 * SLOT
 PICKED_PLANES_AT = WORDS_AT[0] + T
-RESID_AT = (W1_AT[0], WORDS_AT[1] - ROW + 1024, WORDS_AT[1] + ROW - 1024, W1_AT[1])
+RESID_AT = (W1_AT[0], W1_AT[1] - ROW + 1024, W1_AT[1] + ROW - 1024, W1_AT[2])
+ROUNDED_AT = 12 * SLOT
 
 
 def tile_list_tabres_none_kernel(tc, tab_words, tab_scales, w1, w2_words, w2_scales, rT, offs, out):
@@ -79,7 +80,6 @@ def tile_list_tabres_none_kernel(tc, tab_words, tab_scales, w1, w2_words, w2_sca
             return block
 
         planes = placed("planes", [P, T], U8, PLANES_AT)
-        w2_plane = tagged("w2_plane", [P, M], U8)
         picked = {}
         w1_codes = [tagged("w1_codes%d" % a, [P, H], U32) for a in range(PASSES)]
         w1_plane = [tagged("w1_plane%d" % a, [P, H], U8) for a in range(PASSES)]
@@ -96,7 +96,8 @@ def tile_list_tabres_none_kernel(tc, tab_words, tab_scales, w1, w2_words, w2_sca
             src = raw[:].rearrange("p j (m t) -> p m j t", t=PACK)
             rounded = []
             for v, pair in enumerate(PAIRS):
-                rounded.append(tagged("w1_bf%d_%d" % (a, v), [P, PACK * H // 2], BF16))
+                name, shape = "w1_bf%d_%d" % (a, v), [P, PACK * H // 2]
+                rounded.append(placed(name, shape, BF16, ROUNDED_AT) if v else tagged(name, shape, BF16))
                 nc.scalar.copy(rounded[v][:].rearrange("p (t m j) -> p m j t", t=2, j=PACK), src[:, :, :, pair[0] : pair[1] + 1])
             for v in range(len(PAIRS)):
                 quantise_w1(a, v * H // 2, H // 2, rounded[v][:])
@@ -126,10 +127,10 @@ def tile_list_tabres_none_kernel(tc, tab_words, tab_scales, w1, w2_words, w2_sca
                     stop=(a == PASSES - 1 and t == PACK - 1),
                 )
 
-        def first_product_by_pairs(a):
-            for pair in PAIRS:
+        def first_product_by_row_sets(a):
+            for t in range(PACK):
                 for c in range(CHUNKS):
-                    first_product(a, c, pair)
+                    first_product(a, c, (t,))
 
         def relu(c):
             u, at = divmod(c, CHUNKS // 2)
@@ -140,7 +141,6 @@ def tile_list_tabres_none_kernel(tc, tab_words, tab_scales, w1, w2_words, w2_sca
             nc.vector.tensor_copy(picked[a][:, first : first + count], words[:].indirect(listed(first, count)))
 
         nc.vector.memset(planes[:].bitcast(I32), 0)
-        nc.vector.memset(w2_plane[:].bitcast(I32), 0)
         words = load_words(0)
         nc.sync.dma_start(offsets[:], offs)
         for q in range(QUADRANTS):
@@ -153,14 +153,14 @@ def tile_list_tabres_none_kernel(tc, tab_words, tab_scales, w1, w2_words, w2_sca
         picked_planes = placed("picked_planes", [P, S], U8, PICKED_PLANES_AT)
         nc.vector.tensor_copy(picked_planes[:], planes[:].indirect(offsets[:]))
         prepare_w1_on_scalar(0, raw)
-        first_product_by_pairs(0)
+        first_product_by_row_sets(0)
 
         words = load_words(1)
         raw = load_w1(1)
         picked[1] = tagged("w1_bf0_0", [P, S], U32)
         gather_words(1, words, 0, S)
         prepare_w1_shared(1, raw, len(PAIRS))
-        first_product_by_pairs(1)
+        first_product_by_row_sets(1)
 
         prepare_w1_shared(2, load_w1(2), 1)
         picked[2] = tagged("picked2", [P, S], U32)
@@ -173,7 +173,9 @@ def tile_list_tabres_none_kernel(tc, tab_words, tab_scales, w1, w2_words, w2_sca
             relu(c)
 
         resid = [load_resid(0)]
-        w2_codes = tagged("w1_bf0_1", [P, 2 * M], U8)
+        w2_codes = placed("w2_codes", [P, 2 * M], U8, ROUNDED_AT)
+        w2_plane = placed("w2_plane", [P, M], U8, ROUNDED_AT + 2 * M)
+        nc.gpsimd.memset(w2_plane[:].bitcast(I32), 0)
         nc.sync.dma_start(out=w2_codes[:].bitcast(I32), in_=w2_words[0].bitcast(I32))
         for q in range(QUADRANTS):
             nc.sync.dma_start(out=w2_plane[32 * q : 32 * q + 4, :].bitcast(I32), in_=w2_scales[0, 4 * q : 4 * q + 4, :].bitcast(I32))
@@ -206,7 +208,9 @@ def tile_list_tabres_none_kernel(tc, tab_words, tab_scales, w1, w2_words, w2_sca
             queue.dma_start(out=out[P * n : P * (n + 1), first : first + count], in_=res[:])
 
         identity = tagged("identity", [P, P], F32)
+        first_identity = tagged("early1", [P, P], F32)
         make_identity(nc, identity[:])
+        make_identity(nc, first_identity[:])
 
         def stage(n, u, count=HALF):
             staged[n, u] = tagged("staged%d_%d" % (n, u), [P, HALF], F32)
@@ -226,7 +230,7 @@ def tile_list_tabres_none_kernel(tc, tab_words, tab_scales, w1, w2_words, w2_sca
         def add_turned(u, first, term, start=False, stop=False):
             for b, square in enumerate(term):
                 nc.tensor.matmul(
-                    turned[u][:, P * (first + b) : P * (first + b + 1)], square, identity[:], is_transpose=True,
+                    turned[u][:, P * (first + b) : P * (first + b + 1)], square, (first_identity if start and (u, b) == (0, 0) else identity)[:], is_transpose=True,
                     start=(start and b == 0), stop=(stop and b == len(term) - 1),
                 )
 
@@ -244,30 +248,30 @@ def tile_list_tabres_none_kernel(tc, tab_words, tab_scales, w1, w2_words, w2_sca
             return res
 
         ahead = EARLY_FIRST // P
-        gather_early(0, EARLY_FIRST, "early")
+        gather_early(0, EARLY_FIRST, "early0")
         quantise_h(0)
         turned[0] = bank("turned0", [P, HALF], 3)
         add_turned(0, 0, [early[b] for b in range(ahead)], start=True)
         for n in (1, 0, 2):
             second_product(n, 0, n)
-        gather_early(EARLY_FIRST, S - EARLY_FIRST, "early")
+        gather_early(EARLY_FIRST, S - EARLY_FIRST, "early1")
         quantise_h(1)
         stage(1, 0)
         gather_and_add(1, 0)
         turned[1] = bank("turned1", [P, HALF], 1)
         add_turned(1, 0, [early[b] for b in range(HALF // P, S // P)], start=True)
         stage(0, 0)
-        second_product(0, 1, 4)
         second_product(2, 1, 6)
+        second_product(0, 1, 4)
         add_turned(0, 0, squares(staged[0, 0]), stop=True)
         stage(2, 0)
         gather_and_add(2, 0)
+        stage(2, 1)
+        gather_and_add(2, 1)
         stage(0, 1)
         add_turned(1, 0, squares(staged[0, 1]), stop=True)
         second_product(1, 1, 5)
         second_product(3, 0, 0)
-        stage(2, 1)
-        gather_and_add(2, 1)
         turn_back(0, 2)
         stage(1, 1)
         gather_and_add(1, 1, tag="staged2_0")

@@ -183,8 +183,11 @@ def tile_list_tabres_none_kernel(tc, tab_words, tab_scales, w1, w2_words, w2_sca
 
         y, staged, early, turned, back = {}, {}, {}, {}, {}
 
-        def quantise_h(u):
-            nc.vector.quantize_mx(out=h_codes[u][:].bitcast(FP8X4), scales=h_plane[u][:], in_=h_bf[u][:])
+        def quantise_h(u, count=HALF):
+            for first in range(0, HALF, count):
+                cols = slice(first, first + count)
+                rounded = h_bf[u][:, PACK * first : PACK * (first + count)]
+                nc.vector.quantize_mx(out=h_codes[u][:, cols].bitcast(FP8X4), scales=h_plane[u][:, cols], in_=rounded)
 
         def second_product(n, u, index):
             y[n, u] = bank("y%d_%d" % (n, u), [P, HALF], index)
@@ -212,17 +215,16 @@ def tile_list_tabres_none_kernel(tc, tab_words, tab_scales, w1, w2_words, w2_sca
         make_identity(nc, identity[:])
         make_identity(nc, first_identity[:])
 
-        def stage(n, u, count=HALF):
-            staged[n, u] = tagged("staged%d_%d" % (n, u), [P, HALF], F32)
-            for first in range(0, HALF, count):
-                nc.scalar.copy(staged[n, u][:, first : first + count], y[n, u][:, first : first + count])
+        def stage(n, u, first=0, count=HALF):
+            if first == 0:
+                staged[n, u] = tagged("staged%d_%d" % (n, u), [P, HALF], F32)
+            nc.scalar.copy(staged[n, u][:, first : first + count], y[n, u][:, first : first + count])
 
-        def gather_and_add(n, u, count=HALF, tag=None):
-            for done in range(0, HALF, count):
-                res = tagged(tag or "res%d_%d_%d" % (n, u, done), [P, count], F32)
-                first = HALF * u + done
-                nc.vector.tensor_tensor(res[:], resid[n][:].indirect(listed(first, count)), staged[n, u][:, done : done + count], ADD)
-                store(nc.sync, n, first, count, res)
+        def gather_and_add(n, u, first=0, count=HALF, tag=None):
+            res = tagged(tag or "res%d_%d_%d" % (n, u, first), [P, count], F32)
+            token = HALF * u + first
+            nc.vector.tensor_tensor(res[:], resid[n][:].indirect(listed(token, count)), staged[n, u][:, first : first + count], ADD)
+            store(nc.sync, n, token, count, res)
 
         def squares(tile):
             return [tile[:, P * b : P * (b + 1)] for b in range(HALF // P)]
@@ -255,7 +257,7 @@ def tile_list_tabres_none_kernel(tc, tab_words, tab_scales, w1, w2_words, w2_sca
         for n in (1, 0, 2):
             second_product(n, 0, n)
         gather_early(EARLY_FIRST, S - EARLY_FIRST, "early1")
-        quantise_h(1)
+        quantise_h(1, QUARTER)
         stage(1, 0)
         gather_and_add(1, 0)
         turned[1] = bank("turned1", [P, HALF], 1)
@@ -281,6 +283,8 @@ def tile_list_tabres_none_kernel(tc, tab_words, tab_scales, w1, w2_words, w2_sca
         gather_and_add(3, 0)
         results = [fetch_turned(u) for u in range(2)]
         store(nc.scalar, 0, 0, HALF, results[0])
-        stage(3, 1, QUARTER)
+        stage(3, 1, 0, QUARTER)
         store(nc.scalar, 0, HALF, HALF, results[1])
-        gather_and_add(3, 1, QUARTER)
+        gather_and_add(3, 1, 0, QUARTER)
+        stage(3, 1, QUARTER, QUARTER)
+        gather_and_add(3, 1, QUARTER, QUARTER)

@@ -53,10 +53,10 @@ def tile_list_tabres_none_kernel(tc, tab_words, tab_scales, w1, w2_words, w2_sca
         offsets = keep.tile([P, S // GROUP], U16, name="offsets")
 
         def placed(name, shape, dtype, at):
-            return arena.tile(shape, dtype, name=name, tag=name, align_bytes=64, offset=at)
+            return arena.tile(shape, dtype, name=name, tag=name, align_bytes=256, offset=at)
 
         def tagged(tag, shape, dtype):
-            return keep.tile(shape, dtype, name=tag, tag=tag, align_bytes=64)
+            return keep.tile(shape, dtype, name=tag, tag=tag, align_bytes=256)
 
         def bank(name, shape, index):
             return psum.tile(shape, F32, name=name, tag="bank%d" % index)

@@ -140,7 +140,7 @@ def tile_list_tabres_none_kernel(tc, tab_words, tab_scales, w1, w2_words, w2_sca
         def gather_words(a, words, first, count):
             nc.vector.tensor_copy(picked[a][:, first : first + count], words[:].indirect(listed(first, count)))
 
-        nc.vector.memset(planes[:].bitcast(I32), 0)
+        nc.gpsimd.memset(planes[:].bitcast(I32), 0)
         words = load_words(0)
         nc.sync.dma_start(offsets[:], offs)
         for q in range(QUADRANTS):

@@ -39,7 +39,8 @@ WORDS_AT = (SLOT, 6 * SLOT, 10 * SLOT)
 W1_AT = (4 * SLOT, 8 * SLOT, 11 * SLOT)
 PLANES_AT = 3 * SLOT
 PICKED_PLANES_AT = WORDS_AT[0] + T
-RESID_AT = (W1_AT[0], W1_AT[1] - ROW + 1024, W1_AT[1] + ROW - 1024, W1_AT[2])
+W2_PLANE_AT = WORDS_AT[0] + 2 * T
+RESID_AT = (13 * SLOT, W1_AT[1] - ROW + 1024, W1_AT[1] + ROW - 1024, W1_AT[2])
 ROUNDED_AT = 12 * SLOT
 
 
@@ -173,8 +174,8 @@ def tile_list_tabres_none_kernel(tc, tab_words, tab_scales, w1, w2_words, w2_sca
             relu(c)
 
         resid = [load_resid(0)]
-        w2_codes = placed("w2_codes", [P, 2 * M], U8, ROUNDED_AT)
-        w2_plane = placed("w2_plane", [P, M], U8, ROUNDED_AT + 2 * M)
+        w2_codes = tagged("w2_codes", [P, 2 * M], U8)
+        w2_plane = placed("w2_plane", [P, M], U8, W2_PLANE_AT)
         nc.gpsimd.memset(w2_plane[:].bitcast(I32), 0)
         nc.sync.dma_start(out=w2_codes[:].bitcast(I32), in_=w2_words[0].bitcast(I32))
         for q in range(QUADRANTS):

from contextlib import ExitStack

import concourse.mybir as mybir
from concourse.masks import make_identity

K, H, M, T, S = 1536, 512, 512, 2048, 1024
FLOPS = 2 * K * H * S + 2 * H * M * S

F32 = mybir.dt.float32
BF16 = mybir.dt.bfloat16
I32 = mybir.dt.int32
U32 = mybir.dt.uint32
U16 = mybir.dt.uint16
U8 = mybir.dt.uint8
FP8X4 = mybir.dt.float8_e4m3fn_x4
FP4X4 = mybir.dt.float4_e2m1fn_x4
RELU = mybir.ActivationFunctionType.Relu
ADD = mybir.AluOpType.add

P = 128
PACK = 4
PASS = P * PACK
PASSES = K // PASS
QUADRANTS = 4
GROUP = 16
CHUNK = 128
CHUNKS = S // CHUNK
HALF = S // 2
QUARTER = S // 4
PAIRS = ((0, 1), (2, 3))

VECTOR_CASTS = {1: 48, 2: 56}

EARLY_FIRST = 512

ROW = 4 * T
SLOT = ROW + T
WORDS_AT = (SLOT, 6 * SLOT, 10 * SLOT)
W1_AT = (4 * SLOT, 8 * SLOT, 11 * SLOT)
PLANES_AT = 3 * SLOT
PICKED_PLANES_AT = WORDS_AT[0] + T
W2_PLANE_AT = WORDS_AT[0] + 2 * T
RESID_AT = (13 * SLOT, W1_AT[1] - ROW + 1024, W1_AT[1] + ROW - 1024, W1_AT[2])
ROUNDED_AT = 12 * SLOT


def tile_list_tabres_none_kernel(tc, tab_words, tab_scales, w1, w2_words, w2_scales, rT, offs, out):
    nc = tc.nc
    with ExitStack() as ctx:
        keep = ctx.enter_context(tc.tile_pool(name="keep", bufs=1))
        psum = ctx.enter_context(tc.psum_pool(name="psum", bufs=1))
        arena = ctx.enter_context(tc.tile_pool(name="arena", bufs=1))

        offsets = keep.tile([P, S // GROUP], U16, name="offsets")

        def placed(name, shape, dtype, at):
            return arena.tile(shape, dtype, name=name, tag=name, align_bytes=256, offset=at)

        def tagged(tag, shape, dtype):
            return keep.tile(shape, dtype, name=tag, tag=tag, align_bytes=256)

        def bank(name, shape, index):
            return psum.tile(shape, F32, name=name, tag="bank%d" % index)

        def listed(first, count):
            return offsets[:, first // GROUP : (first + count) // GROUP]

        def load_w1(a):
            raw = placed("w1_raw%d" % a, [P, PACK, H], F32, W1_AT[a])
            nc.sync.dma_start(out=raw[:], in_=w1[PASS * a : PASS * (a + 1), :].rearrange("(p j) c -> p j c", j=PACK))
            return raw

        def load_words(a):
            words = placed("words%d" % a, [P, T], U32, WORDS_AT[a])
            nc.sync.dma_start(out=words[:].bitcast(I32), in_=tab_words[a].rearrange("p t i -> p (t i)").bitcast(I32))
            return words

        def load_resid(n):
            block = placed("resid%d" % n, [P, T], F32, RESID_AT[n])
            nc.sync.dma_start(out=block[:], in_=rT[P * n : P * (n + 1), :])
            return block

        planes = placed("planes", [P, T], U8, PLANES_AT)
        picked = {}
        w1_codes = [tagged("w1_codes%d" % a, [P, H], U32) for a in range(PASSES)]
        w1_plane = [tagged("w1_plane%d" % a, [P, H], U8) for a in range(PASSES)]
        h_bf = [tagged("h_bf%d" % u, [P, HALF * PACK], BF16) for u in range(2)]
        h_codes = [tagged("h_codes%d" % u, [P, HALF], U32) for u in range(2)]
        h_plane = [tagged("h_plane%d" % u, [P, HALF], U8) for u in range(2)]
        h_sum = [bank("bank%d" % c, [P, PACK, CHUNK], c) for c in range(CHUNKS)]

        def quantise_w1(a, first, count, rounded):
            cols = slice(first, first + count)
            nc.vector.quantize_mx(out=w1_codes[a][:, cols].bitcast(FP8X4), scales=w1_plane[a][:, cols], in_=rounded)

        def prepare_w1_on_scalar(a, raw):
            src = raw[:].rearrange("p j (m t) -> p m j t", t=PACK)
            rounded = []
            for v, pair in enumerate(PAIRS):
                name, shape = "w1_bf%d_%d" % (a, v), [P, PACK * H // 2]
                rounded.append(placed(name, shape, BF16, ROUNDED_AT) if v else tagged(name, shape, BF16))
                nc.scalar.copy(rounded[v][:].rearrange("p (t m j) -> p m j t", t=2, j=PACK), src[:, :, :, pair[0] : pair[1] + 1])
            for v in range(len(PAIRS)):
                quantise_w1(a, v * H // 2, H // 2, rounded[v][:])

        def prepare_w1_shared(a, raw, pieces):
            rounded = tagged("w1_bf%d" % a, [P, PACK * H], BF16)
            src = raw[:].rearrange("p j (m t) -> p m j t", t=PACK)
            dst = rounded[:].rearrange("p (t m j) -> p m j t", t=PACK, j=PACK)
            split = VECTOR_CASTS[a]
            nc.vector.tensor_copy(dst[:, :split], src[:, :split])
            nc.scalar.copy(dst[:, split:], src[:, split:])
            width = H // pieces
            for first in range(0, H, width):
                quantise_w1(a, first, width, rounded[:, PACK * first : PACK * (first + width)])

        def first_product(a, c, row_sets):
            cols = slice(CHUNK * c, CHUNK * (c + 1))
            for t in row_sets:
                wcols = slice(P * t, P * (t + 1))
                nc.tensor.matmul_mx(
                    out=h_sum[c][:, t, :],
                    lhsT=w1_codes[a][:, wcols].bitcast(FP8X4),
                    lhsT_scale=w1_plane[a][:, wcols],
                    rhs=picked[a][:, cols].bitcast(FP8X4),
                    rhs_scale=picked_planes[4 * a : P, cols],
                    start=(a == 0 and t == 0),
                    stop=(a == PASSES - 1 and t == PACK - 1),
                )

        def first_product_by_row_sets(a):
            for t in range(PACK):
                for c in range(CHUNKS):
                    first_product(a, c, (t,))

        def relu(c):
            u, at = divmod(c, CHUNKS // 2)
            dst = h_bf[u][:, at * PACK * CHUNK : (at + 1) * PACK * CHUNK].rearrange("p (n t) -> p n t", t=PACK)
            nc.scalar.activation(dst, h_sum[c][:].rearrange("p t n -> p n t"), RELU)

        def gather_words(a, words, first, count):
            nc.vector.tensor_copy(picked[a][:, first : first + count], words[:].indirect(listed(first, count)))

        nc.gpsimd.memset(planes[:].bitcast(I32), 0)
        words = load_words(0)
        nc.sync.dma_start(offsets[:], offs)
        for q in range(QUADRANTS):
            (nc.sync if q % 2 else nc.scalar).dma_start(
                out=planes[32 * q : 32 * q + 4 * PASSES, :].bitcast(I32), in_=tab_scales[:, 4 * q : 4 * q + 4, :].bitcast(I32)
            )
        raw = load_w1(0)
        picked[0] = tagged("picked0", [P, S], U32)
        gather_words(0, words, 0, S)
        picked_planes = placed("picked_planes", [P, S], U8, PICKED_PLANES_AT)
        nc.vector.tensor_copy(picked_planes[:], planes[:].indirect(offsets[:]))
        prepare_w1_on_scalar(0, raw)
        first_product_by_row_sets(0)

        words = load_words(1)
        raw = load_w1(1)
        picked[1] = tagged("w1_bf0_0", [P, S], U32)
        gather_words(1, words, 0, S)
        prepare_w1_shared(1, raw, len(PAIRS))
        first_product_by_row_sets(1)

        prepare_w1_shared(2, load_w1(2), 1)
        picked[2] = tagged("picked2", [P, S], U32)
        words = load_words(2)
        for first, count in ((0, CHUNK), (CHUNK, CHUNK), (QUARTER, QUARTER), (HALF, HALF)):
            gather_words(2, words, first, count)
            for c in range(first // CHUNK, (first + count) // CHUNK):
                first_product(2, c, range(PACK))
        for c in range(CHUNKS):
            relu(c)

        resid = [load_resid(0)]
        w2_codes = tagged("w2_codes", [P, 2 * M], U8)
        w2_plane = placed("w2_plane", [P, M], U8, W2_PLANE_AT)
        nc.gpsimd.memset(w2_plane[:].bitcast(I32), 0)
        nc.sync.dma_start(out=w2_codes[:].bitcast(I32), in_=w2_words[0].bitcast(I32))
        for q in range(QUADRANTS):
            nc.sync.dma_start(out=w2_plane[32 * q : 32 * q + 4, :].bitcast(I32), in_=w2_scales[0, 4 * q : 4 * q + 4, :].bitcast(I32))
        resid = resid + [load_resid(n) for n in range(1, M // P)]

        y, staged, early, turned, back = {}, {}, {}, {}, {}

        def quantise_h(u, count=HALF):
            for first in range(0, HALF, count):
                cols = slice(first, first + count)
                rounded = h_bf[u][:, PACK * first : PACK * (first + count)]
                nc.vector.quantize_mx(out=h_codes[u][:, cols].bitcast(FP8X4), scales=h_plane[u][:, cols], in_=rounded)

        def second_product(n, u, index):
            y[n, u] = bank("y%d_%d" % (n, u), [P, HALF], index)
            nc.tensor.matmul_mx(
                out=y[n, u][:],
                lhsT=w2_codes[:, 2 * P * n : 2 * P * (n + 1)].bitcast(FP4X4),
                lhsT_scale=w2_plane[:, P * n : P * (n + 1)],
                rhs=h_codes[u][:].bitcast(FP8X4),
                rhs_scale=h_plane[u][:],
                start=True,
                stop=True,
            )

        def gather_early(first, count, tag):
            picked_rows = tagged(tag, [P, count], F32)
            nc.vector.tensor_copy(picked_rows[:], resid[0][:].indirect(listed(first, count)))
            for at in range(0, count, P):
                early[(first + at) // P] = picked_rows[:, at : at + P]

        def store(queue, n, first, count, res):
            queue.dma_start(out=out[P * n : P * (n + 1), first : first + count], in_=res[:])

        identity = tagged("identity", [P, P], F32)
        first_identity = tagged("early1", [P, P], F32)
        make_identity(nc, identity[:])
        make_identity(nc, first_identity[:])

        def stage(n, u, first=0, count=HALF):
            if first == 0:
                staged[n, u] = tagged("staged%d_%d" % (n, u), [P, HALF], F32)
            nc.scalar.copy(staged[n, u][:, first : first + count], y[n, u][:, first : first + count])

        def gather_and_add(n, u, first=0, count=HALF, tag=None):
            res = tagged(tag or "res%d_%d_%d" % (n, u, first), [P, count], F32)
            token = HALF * u + first
            nc.vector.tensor_tensor(res[:], resid[n][:].indirect(listed(token, count)), staged[n, u][:, first : first + count], ADD)
            store(nc.sync, n, token, count, res)

        def squares(tile):
            return [tile[:, P * b : P * (b + 1)] for b in range(HALF // P)]

        def add_turned(u, first, term, start=False, stop=False):
            for b, square in enumerate(term):
                nc.tensor.matmul(
                    turned[u][:, P * (first + b) : P * (first + b + 1)], square, (first_identity if start and (u, b) == (0, 0) else identity)[:], is_transpose=True,
                    start=(start and b == 0), stop=(stop and b == len(term) - 1),
                )

        def turn_back(u, index):
            total = tagged("total%d" % u, [P, HALF], F32)
            nc.scalar.copy(total[:], turned[u][:])
            back[u] = bank("back%d" % u, [P, HALF], index)
            for b in range(HALF // P):
                cols = slice(P * b, P * (b + 1))
                nc.tensor.transpose(back[u][:, cols], total[:, cols], identity[:])

        def fetch_turned(u):
            res = tagged("res0_%d" % u, [P, HALF], F32)
            nc.scalar.copy(res[:], back[u][:])
            return res

        ahead = EARLY_FIRST // P
        gather_early(0, EARLY_FIRST, "early0")
        quantise_h(0)
        turned[0] = bank("turned0", [P, HALF], 3)
        add_turned(0, 0, [early[b] for b in range(ahead)], start=True)
        for n in (1, 0, 2):
            second_product(n, 0, n)
        gather_early(EARLY_FIRST, S - EARLY_FIRST, "early1")
        quantise_h(1, QUARTER)
        stage(1, 0)
        gather_and_add(1, 0)
        turned[1] = bank("turned1", [P, HALF], 1)
        add_turned(1, 0, [early[b] for b in range(HALF // P, S // P)], start=True)
        stage(0, 0)
        second_product(2, 1, 6)
        second_product(0, 1, 4)
        add_turned(0, 0, squares(staged[0, 0]), stop=True)
        stage(2, 0)
        gather_and_add(2, 0)
        stage(2, 1)
        gather_and_add(2, 1)
        stage(0, 1)
        add_turned(1, 0, squares(staged[0, 1]), stop=True)
        second_product(1, 1, 5)
        second_product(3, 0, 0)
        turn_back(0, 2)
        stage(1, 1)
        gather_and_add(1, 1, tag="staged2_0")
        turn_back(1, 4)
        second_product(3, 1, 7)
        stage(3, 0)
        gather_and_add(3, 0)
        results = [fetch_turned(u) for u in range(2)]
        store(nc.scalar, 0, 0, HALF, results[0])
        stage(3, 1, 0, QUARTER)
        store(nc.scalar, 0, HALF, HALF, results[1])
        gather_and_add(3, 1, 0, QUARTER)
        stage(3, 1, QUARTER, QUARTER)
        gather_and_add(3, 1, QUARTER, QUARTER)
